import numpy as np, ml_dtypes
CORES = [3,7,11,15,131,135,139,143]
N = 8
import mx_ref
BF = ml_dtypes.bfloat16
def cols(t, e):
    v = np.concatenate([t.reshape(128, -1, 4), np.zeros((128, 1, 4), BF)], axis=1)
    return np.ascontiguousarray(v[:, e]).reshape(128, -1)
def cut(t, i, w=512):
    return t[:, w * i:w * i + w]
def pick(q, e):
    c = np.concatenate([q[0].reshape(128, -1, 4), np.zeros((128, 1, 4), np.uint8)], axis=1); s = np.concatenate([q[1], np.ones((16, 1), np.uint8)], axis=1)
    return (np.ascontiguousarray(c[:, e].reshape(128, -1)), np.ascontiguousarray(s[:, e]))
def join(*qs):
    return (np.concatenate([q[0] for q in qs], axis=1), np.concatenate([q[1] for q in qs], axis=1))
def put(q, e, v):
    c, s = q[0].reshape(128, -1, 4).copy(), q[1].copy(); c[:, e] = v[0].reshape(128, -1, 4); s[:, e] = v[1]
    return (c.reshape(128, -1), s)
def pk(c, s):
    return (np.ascontiguousarray(c), mx_ref.live(s))
def emit(q):
    return q[0], q[1]
def decode(q):
    o = []
    for b in range(4):
        e = np.zeros((128, 128, 4), np.float32); e[np.arange(128), np.arange(128), b] = 1
        o.append(mx_ref.matmul(mx_ref.quantize(e.reshape(128, 512).astype(BF)), q))
    return np.stack(o, axis=2).reshape(128, -1)
def f(rng, *shape):
    return mx_ref.flush((rng.standard_normal(shape, dtype=np.float32) * np.exp2(rng.integers(-2, 3, shape[:-1] + (1,)))).astype(BF))
def wide(rng, *shape, cols=0):
    v = rng.standard_normal(shape, dtype=np.float32) * np.exp2(rng.integers(-12, 13, shape)).astype(np.float32)
    if cols: v *= np.repeat(np.exp2(rng.integers(-cols, cols + 1, shape[:-2] + (1, shape[-1] // 4))) * (rng.random(shape[:-2] + (1, shape[-1] // 4)) > 0.0625), 4, axis=-1).astype(np.float32)
    return mx_ref.flush(v.astype(BF))
T, C = 128, 32
def best(s):
    return np.argsort(-(s + np.float32(0)), kind="stable")[:C]
def quant(u, v):
    qu = [mx_ref.quantize(np.ascontiguousarray(u[r])) for r in range(N)]
    return qu, [[mx_ref.quantize(np.ascontiguousarray(cut(v[r], i))) for i in range(4)] for r in range(N)]
def layer(q, qu, qv):
    e = best(mx_ref.matmul(qu, q)[0])
    old = pick(q, e)
    a = np.stack([mx_ref.matmul(t, old) for t in qv], axis=2)
    new = np.maximum(a, np.float32(0)) * np.float32(0.05) + decode(old).reshape(128, C, 4)
    return e, new.reshape(128, -1).astype(BF)
def setup_inputs(rng):
    u = np.zeros((N, 128, 512), BF)
    u[:, :, :4] = f(rng, N, 128, 4)
    return {"x": f(rng, N, 128, 4 * T), "u": u, "v": f(rng, N, 128, 2048), "w": f(rng, N, 128, 512)}
def setup_inputs_spread(rng):
    d = setup_inputs(rng)
    d["x"] = wide(rng, N, 128, 4 * T, cols=3)
    return d
def setup_inputs_ties(rng):
    d = setup_inputs(rng)
    d["x"] = np.stack([cols(d["x"][r], rng.permutation(T) % 5 - 1) for r in range(N)])
    d["u"][1::2] = 0
    return d
def setup_inputs_again(rng):
    d = setup_inputs(rng)
    x, u = d["x"].astype(np.float32).reshape(N, 128, T, 4), np.zeros((N, 128, 512), np.float32)
    good = np.stack([rng.permutation(T) < C for r in range(N)])
    x[:, :32] = (1 + rng.random((N, 32, T, 4))) * np.where(good, 1.0, -1.0)[:, None, :, None]
    u[:, :32, :4] = 1 + rng.random((N, 32, 4))
    d["x"], d["u"] = x.reshape(N, 128, 4 * T).astype(BF), u.astype(BF)
    return d
def setup_inputs_other(rng):
    d = setup_inputs(rng)
    x, u = d["x"].astype(np.float32).reshape(N, 128, T, 4), np.zeros((N, 128, 512), np.float32)
    v = d["v"].astype(np.float32).reshape(N, 128, 4, 128, 4)
    large = np.stack([rng.permutation(T) < C for r in range(N)])
    x[:, :16] = (1 + rng.random((N, 16, T, 4))) * np.where(large, 16.0, 1.0)[:, None, :, None]
    x[:, 16:32] = (0.25 + 0.25 * rng.random((N, 16, T, 4))) * rng.choice([-1.0, 1.0], (N, 16, T, 4))
    u[:, :16, :4] = 1 + rng.random((N, 16, 4))
    u[:, 16:32, :4] = -1 - rng.random((N, 16, 4))
    v[:, :, :, 16:32] = 0
    v[:, :16, :, 16:32] = 256 * (1 + rng.random((N, 16, 4, 16, 4)))
    d["x"], d["u"], d["v"] = x.reshape(N, 128, 4 * T).astype(BF), u.astype(BF), v.reshape(N, 128, 2048).astype(BF)
    return d
def setup_inputs_neg(rng):
    d = setup_inputs(rng)
    d["x"] = np.abs(d["x"].astype(np.float32)).astype(BF)
    d["v"] = (-np.abs(d["v"].astype(np.float32))).astype(BF)
    return d
def check_inputs(d):
    b = []
    for k in ("x", "u", "v", "w"):
        a = np.abs(d[k].astype(np.float32))
        if not (np.isfinite(a).all() and ((a == 0) | (a >= 2.0 ** -30) & (a <= 2.0 ** 30)).all()): b.append("a value of " + k)
    if (d["u"][:, :, 4:].astype(np.float32) != 0).any(): b.append("u has numbers behind its column 0")
    if b: return b
    qu, qv = quant(d["u"], d["v"])
    for r in range(N):
        q = mx_ref.quantize(np.ascontiguousarray(d["x"][r]))
        for k in (1, 2):
            e, new = layer(q, qu[(r + k) % N], qv[(r + k) % N])
            a = np.abs(new.astype(np.float32)).reshape(16, 8, C, 4).max(axis=(1, 3))
            if not ((a == 0) | (a >= 2.0 ** -30) & (a <= 2.0 ** 30)).all(): return ["a number of a made column"]
            q = put(q, e, mx_ref.quantize(new))
    return b
def reference(x, u, v, w):
    oc, osc = np.zeros((N, 128, 4 * T), np.uint8), np.zeros((N, 16, T), np.uint8)
    li, y = np.zeros((N, 2, C), np.float32), np.zeros((N, 128, T), np.float32)
    qu, qv = quant(u, v)
    for d in range(N):
        r = (d - 2) % N
        q = mx_ref.quantize(np.ascontiguousarray(x[r]))
        for k in (1, 2):
            s = (r + k) % N
            e, new = layer(q, qu[s], qv[s])
            q = put(q, e, mx_ref.quantize(new))
            li[d, k - 1] = e
        oc[d], osc[d] = emit(q)
        y[d] = mx_ref.matmul(mx_ref.quantize(np.ascontiguousarray(w[d])), q)
    return {"oc": oc, "osc": osc, "li": li, "y": y}

@@ -1,0 +1,310 @@
+from concourse.bass import DstId, RemoteDMATransfer
+from concourse.mybir import dt, AluOpType, ActivationFunctionType
+
+N = 8
+C = 32
+FACTOR = 13421773 * 2.0 ** -28
+FAR = 1.0e29
+
+CODE = "float8_e4m3fn_x4"
+SCRATCH = {
+    "xb": ("sbuf", [128, 512], "bfloat16"), "ub": ("sbuf", [128, 512], "bfloat16"),
+    "vb": ("sbuf", [128, 2048], "bfloat16"), "wb": ("sbuf", [128, 512], "bfloat16"),
+    "zf": ("sbuf", [128, 128], "float32"), "ob": ("sbuf", [128, 128], "bfloat16"),
+    "idn": ("sbuf", [128, 128], "bfloat16"), "eb": ("sbuf", [128, 520], "bfloat16"),
+    "wo": ("sbuf", [128, 512], "bfloat16"), "later": ("sbuf", [128, 128], "float32"),
+    "jm": ("sbuf", [128, 128], "float32"), "gs": ("sbuf", [128, 128], "float32"),
+    "pif": ("sbuf", [128, 1], "float32"), "pii": ("sbuf", [128, 1], "int32"), "pmi": ("sbuf", [128, 1], "int32"),
+    "pm0": ("sbuf", [128, 1], "float32"), "pm1": ("sbuf", [128, 1], "float32"),
+    "thr": ("sbuf", [128, 128], "bfloat16"), "km": ("sbuf", [128, 128], "bfloat16"),
+    "cr": ("sbuf", [128, 128], "bfloat16"), "ca": ("sbuf", [128, 128], "bfloat16"), "cb": ("sbuf", [128, 128], "bfloat16"),
+    "on": ("sbuf", [128, 256], "bfloat16"), "z8": ("sbuf", [128, 8], "uint16"),
+    "j16": ("sbuf", [128, 8], "float32"), "j8": ("sbuf", [128, 8], "float32"), "jr": ("sbuf", [128, 8], "float32"),
+    "qx": ("sbuf", [128, 128], CODE), "sx": ("sbuf", [128, 128], "uint8"),
+    "qu": ("sbuf", [128, 128], CODE), "su": ("sbuf", [128, 128], "uint8"),
+    "qv": ("sbuf", [128, 512], CODE), "sv": ("sbuf", [128, 512], "uint8"),
+    "qw": ("sbuf", [128, 128], CODE), "sw": ("sbuf", [128, 128], "uint8"),
+    "qe": ("sbuf", [128, 512], CODE), "se": ("sbuf", [128, 512], "uint8"),
+    "qo": ("sbuf", [128, 128], CODE), "so": ("sbuf", [128, 128], "uint8"),
+    "ur": ("sbuf", [128, 128], CODE), "urs": ("sbuf", [128, 128], "uint8"),
+    "up": ("sbuf", [128, 128], CODE), "ups": ("sbuf", [128, 128], "uint8"),
+    "tu": ("sbuf", [128, 8], CODE), "tus": ("sbuf", [128, 32], "uint8"),
+    "ta": ("sbuf", [128, 128], CODE), "tas": ("sbuf", [128, 128], "uint8"),
+    "tb": ("sbuf", [128, 160], CODE), "tbs": ("sbuf", [128, 160], "uint8"),
+    "sm": ("sbuf", [128, 128], "float32"),
+    "h1": ("sbuf", [128, 512], "bfloat16"), "h3": ("sbuf", [128, 512], "bfloat16"),
+    "qh1": ("sbuf", [128, 128], CODE), "sh1": ("sbuf", [128, 128], "uint8"),
+    "qh2": ("sbuf", [128, 128], CODE), "sh2": ("sbuf", [128, 128], "uint8"),
+    "qh3": ("sbuf", [128, 128], CODE), "sh3": ("sbuf", [128, 128], "uint8"),
+    "nb": ("sbuf", [128, 256], "bfloat16"), "sc": ("sbuf", [128, 256], "bfloat16"),
+    "lst": ("sbuf", [128, 2], "uint16"),
+    "mk": ("sbuf", [128, 128], "bfloat16"), "r8": ("sbuf", [128, 128], "bfloat16"),
+    "c8": ("sbuf", [128, 8], "float32"), "d8": ("sbuf", [128, 8], "float32"), "e8": ("sbuf", [128, 8], "float32"),
+    "f8": ("sbuf", [128, 8], "float32"), "off1": ("sbuf", [128, 8], "uint16"),
+    "fl": ("sbuf", [128, 128], "bfloat16"), "st": ("sbuf", [128, 128], "bfloat16"), "off2": ("sbuf", [128, 8], "uint16"),
+    "nl": ("sbuf", [128, 128], "bfloat16"), "sl": ("sbuf", [128, 128], "bfloat16"),
+    "li0": ("sbuf", [128, 1], "float32"), "li1": ("sbuf", [128, 1], "float32"),
+    "ra": ("sbuf", [128, 512], "float32"), "rb": ("sbuf", [128, 512], "float32"),
+    "n1": ("sbuf", [128, 512], "bfloat16"), "n2": ("sbuf", [128, 512], "bfloat16"),
+    "qn": ("sbuf", [128, 128], CODE), "sn": ("sbuf", [128, 128], "uint8"),
+    "pk": ("sbuf", [128, 32], CODE), "pks": ("sbuf", [128, 32], "uint8"),
+    "win": ("sbuf", [128, 256], CODE), "wins": ("sbuf", [128, 256], "uint8"),
+    "t2": ("sbuf", [128, 128], CODE), "t2s": ("sbuf", [128, 128], "uint8"),
+    "ys": ("sbuf", [128, 128], "float32"),
+}
+for _i in range(8):
+    SCRATCH["p%d" % _i] = ("psum", [128, 512], "float32")
+
+LOADS = ["dx", "du", "dv0", "dv1", "dw"]
+STORES = ["do", "ds0", "ds1", "ds2", "ds3", "dy", "dl0", "dl1"]
+SEMAPHORES = ["cv", "cs", "ct", "cg", "sent", "arru", "arra", "arrb", "arrn"] + LOADS + STORES
+
+
+def rank_program(g, core, T, topo):
+    rank = T.rank_of(core)
+    if rank is None:
+        return
+    A, F = AluOpType, ActivationFunctionType
+    queue = {"v": g.vector, "s": g.scalar, "t": g.tensor, "g": g, "y": g.sync}
+    counter = {"v": "cv", "s": "cs", "t": "ct", "g": "cg"}
+    count = {"v": 0, "s": 0, "t": 0, "g": 0}
+    known = {q: {} for q in queue}
+    wrote, read = {}, {}
+    order = [0]
+
+    def ready(q, reads, writes):
+        need = [wrote[k] for k in list(reads) + list(writes) if k in wrote]
+        for k in writes:
+            need += read.get(k, [])
+        for _, name, val, kn in sorted(need, key=lambda e: -e[0]):
+            if known[q].get(name, 0) < val:
+                queue[q].wait_ge(T.sem[name], val)
+                known[q][name] = val
+            for n2, v2 in kn.items():
+                known[q][n2] = max(known[q].get(n2, 0), v2)
+
+    def done(q, ev, reads, writes):
+        for k in reads:
+            read.setdefault(k, []).append(ev)
+        for k in writes:
+            wrote[k] = ev
+            read[k] = []
+
+    def op(q, reads, writes, call, *args, **kw):
+        ready(q, reads, writes)
+        count[q] += 1
+        order[0] += 1
+        call(*args, **kw).then_inc(T.sem[counter[q]], 1)
+        done(q, (order[0], counter[q], count[q], dict(known[q])), reads, writes)
+
+    def dma(q, sem, reads, writes, out, in_):
+        ready(q, reads, writes)
+        order[0] += 1
+        queue[q].dma_start(out, in_).then_inc(T.sem[sem], 16)
+        done(q, (order[0], sem, 16, dict(known[q])), reads, writes)
+
+    V, S, E = g.vector, g.scalar, g.tensor
+    nxt, nxt2 = T.cores[(rank + 1) % N], T.cores[(rank + 2) % N]
+
+    def lanes(dst):
+        return topo.engines(core, dst)[:8]
+
+    def bits(es):
+        return sum(1 << e for e in es)
+
+    def send(reads, dst, out, in_, sem):
+        ready("g", reads, [])
+        rid, pid = topo.addr(dst, core)
+        g.remote_dma(out_ap=out, in_ap=in_, remote_sem=T.sem[sem], local_sem=T.sem.sent, pid=pid, routing_id=rid,
+                     dma_engine_mask=bits(lanes(dst)))
+
+    def lane_count(src, dst):
+        return len(topo.engines(src, dst)[:8])
+
+    me = core
+    prv, prv2 = T.cores[(rank - 1) % N], T.cores[(rank - 2) % N]
+    land = {"tu": ("arru", lane_count(prv, me)), "ta": ("arra", 2 * lane_count(prv, me)),
+            "tb": ("arrb", 2 * lane_count(prv2, me)), "tn": ("arrn", 2 * lane_count(prv, me))}
+    for k, (s, n) in land.items():
+        wrote[k] = (0, s, n, {})
+
+    def code(name, a, b):
+        return T[name][:, a:b].bitcast(dt.uint8)
+
+    def word(name, a, b):
+        return T[name][:, a:b].bitcast(dt.uint32)
+
+    dma("s", "du", [], ["u"], T.ub[:, 0:8], T.u[:, 0:8])
+    dma("y", "dx", [], ["x"], T.xb[:], T.x[:, 0:512])
+    dma("y", "dv0", [], ["v0"], T.vb[:, 0:1024], T.v[:, 0:1024])
+    dma("y", "dv1", [], ["v1"], T.vb[:, 1024:2048], T.v[:, 1024:2048])
+    dma("s", "dw", [], ["w"], T.wb[:], T.w[:, 0:512])
+
+    op("v", [], ["ob"], V.memset, T.ob[:], 1.0)
+    op("v", [], ["zf"], V.memset, T.zf[:], 0.0)
+    op("g", ["ob"], ["idn"], g.affine_select, T.idn[:], T.ob[:], [[-1, 128]], A.is_equal, 0.0, 0, 1)
+    op("g", ["zf"], ["later"], g.affine_select, T.later[:], T.zf[:], [[1, 128]], A.is_gt, FAR, 0, -1)
+    op("g", [], ["pii"], g.iota, T.pii[:], [[0, 1]], 0, 1)
+    op("g", [], ["pif"], g.iota, T.pif[:], [[0, 1]], 0, 1, allow_small_or_imprecise_dtypes=True)
+    op("g", [], ["jm"], g.iota, T.jm[:], [[0, 8], [1, 16]], 0, 0, allow_small_or_imprecise_dtypes=True)
+    op("g", [], ["j16"], g.iota, T.j16[:], [[16, 8]], 0, 0, allow_small_or_imprecise_dtypes=True)
+    op("v", [], ["uz"], V.memset, T.ub[:, 8:512], 0.0)
+    op("v", [], ["eb"], V.memset, T.eb[:], 0.0)
+    op("v", ["idn"], ["eb"], V.tensor_copy, T.eb[:, 3:515:4], T.idn[:])
+    for b in range(4):
+        op("v", ["eb"], ["qe%d" % b], V.quantize_mx, T.qe[:, 128 * b:128 * b + 128], T.se[:, 128 * b:128 * b + 128],
+           T.eb[:, 3 - b:515 - b])
+    op("v", [], ["z8"], V.memset, T.z8[:], 0)
+    op("v", [], ["h1"], V.memset, T.h1[:], 0.0)
+
+    op("v", ["u", "uz"], ["qu"], V.quantize_mx, T.qu[:], T.su[:], T.ub[:])
+    op("v", ["x"], ["qx"], V.quantize_mx, T.qx[:], T.sx[:], T.xb[:])
+    ready("g", ["qu"], [])
+    rid, pid = topo.addr(nxt, core)
+    es = lanes(nxt)
+    half = len(es) // 2
+    to = [DstId(rid=rid, pnc=pid)]
+    g.remote_dma_fused([
+        RemoteDMATransfer(dst_ids=to, dma_engine_mask=bits(es[:half]), remote_sem=T.sem.arru, src=code("qu", 0, 1), dst=code("tu", 0, 1)),
+        RemoteDMATransfer(dst_ids=to, dma_engine_mask=bits(es[half:]), remote_sem=T.sem.arru, src=T.su[:, 0:4], dst=T.tus[:, 0:4]),
+    ], local_sem=T.sem.sent)
+    send(["qx"], nxt, code("ta", 0, 128), code("qx", 0, 128), "arra")
+    send(["qx"], nxt, T.tas[:, 0:128], T.sx[:, 0:128], "arra")
+    send(["qx"], nxt2, code("tb", 0, 128), code("qx", 0, 128), "arrb")
+    send(["qx"], nxt2, T.tbs[:, 0:128], T.sx[:, 0:128], "arrb")
+    sent = len(es) + 2 * len(es) + 2 * len(lanes(nxt2)) + 2 * len(es)
+
+    def repeat(src, srcs, dst, dsts, key, out):
+        op("v", [key, "z8"], [out], V.tensor_copy, word(dst, 0, 128), word(src, 0, 1).indirect(T.z8[:, 0:8]))
+        op("s", [key, "z8"], [out + "s"], S.activation, T[dsts][:, 0:128], T[srcs][:, 0:1].indirect(T.z8[:, 0:8]), F.Copy)
+
+    repeat("qu", "su", "ur", "urs", "qu", "ur")
+    op("v", ["pii"], ["pmi"], V.tensor_scalar, T.pmi[:], T.pii[:], 15, None, A.bitwise_and)
+    op("v", [], ["wo"], V.memset, T.wo[:], 1.0)
+    op("v", [], ["on"], V.memset, T.on[:], 1.0)
+    op("v", ["pmi"], ["pm0"], V.tensor_copy, T.pm0[:], T.pmi[:])
+    op("v", ["wo"], ["qo"], V.quantize_mx, T.qo[:], T.so[:], T.wo[:])
+    op("v", ["pm0"], ["pm1"], V.tensor_scalar, T.pm1[:], T.pm0[:], 16.0, None, A.add)
+    for i in range(4):
+        op("v", ["v%d" % (i // 2)], ["qv%d" % i], V.quantize_mx, T.qv[:, 128 * i:128 * i + 128], T.sv[:, 128 * i:128 * i + 128],
+           T.vb[:, 512 * i:512 * i + 512])
+    repeat("tu", "tus", "up", "ups", "tu", "up")
+    op("g", [], ["gs"], g.iota, T.gs[:], [[16, 8], [0, 16]], 128, 0, allow_small_or_imprecise_dtypes=True)
+
+    def mm(reads, bank, w, ws, a, x, xs, b, n=128):
+        op("t", reads, [bank], E.matmul_mx, T[bank][:, 0:n], T[w][:, a:a + 128], T[ws][:, a:a + 128],
+           T[x][:, b:b + n], T[xs][:, b:b + n], True, True)
+
+    def scores(u, us, ukeys, t, ts, tk, at):
+        mm(ukeys + tk, "p0", t, ts, at, u, us, 0)
+        mm(ukeys + tk, "p1", u, us, 0, t, ts, at)
+
+    def compare(h, qh, sh):
+        op("v", ["later", "p0"], ["sm"], V.tensor_scalar, T.sm[:], T.later[:], T.p0[:, 0:1], None, A.add)
+        op("v", ["p0", "p1"], [h], V.tensor_scalar, T[h][:, 0:512:4], T.p1[:, 0:128], T.p0[:, 0:1], None, A.is_lt)
+        op("v", ["sm", "p1"], [h + "e"], V.tensor_tensor, T[h][:, 1:512:4], T.p1[:, 0:128], T.sm[:], A.is_equal)
+        op("v", [h, h + "e"], [qh], V.quantize_mx, T[qh][:], T[sh][:], T[h][:])
+
+    def ranks(qh, sh):
+        mm(["qo", qh], "p2", "qo", "so", 0, qh, sh, 0)
+
+    def row(i, bank, t, ts, tk, at):
+        mm(["qv%d" % i] + tk, bank, "qv", "sv", 128 * i, t, ts, at)
+
+    def old(i, bank, t, ts, tk, at):
+        mm(["qe%d" % i] + tk, bank, "qe", "se", 128 * i, t, ts, at)
+
+    def relu(i, bank, r):
+        op("s", [bank], [r + str(i)], S.activation, T[r][:, 128 * i:128 * i + 128], T[bank][:, 0:128], F.Relu, scale=FACTOR)
+
+    def add(i, bank, r, n):
+        op("v", [bank, r + str(i)], [n + str(i)], V.tensor_tensor, T[n][:, i:512:4], T[bank][:, 0:128],
+           T[r][:, 128 * i:128 * i + 128], A.add)
+
+    def first_half(t, ts, tk, at, r, n, h, qh, sh):
+        row(0, "p3", t, ts, tk, at)
+        row(1, "p4", t, ts, tk, at)
+        old(0, "p5", t, ts, tk, at)
+        old(1, "p6", t, ts, tk, at)
+        row(2, "p7", t, ts, tk, at)
+        compare(h, qh, sh)
+        ranks(qh, sh)
+        for i, b in enumerate(["p3", "p4", "p7"]):
+            relu(i, b, r)
+        add(0, "p5", r, n)
+        add(1, "p6", r, n)
+        row(3, "p3", t, ts, tk, at)
+        old(2, "p5", t, ts, tk, at)
+        old(3, "p6", t, ts, tk, at)
+        relu(3, "p3", r)
+
+    def second_half(r, n, q, s, key):
+        add(2, "p5", r, n)
+        add(3, "p6", r, n)
+        op("v", [n + str(i) for i in range(4)], [key], V.quantize_mx, T[q][:, 0:128], T[s][:, 0:128], T[n][:])
+
+    def places(name):
+        op("v", ["p2", "pif"], ["nl"], V.tensor_scalar, T.nl[0:C, :], T.p2[0:C, 0:128], T.pif[0:C, 0:1], None, A.not_equal)
+        op("v", ["nl", "on"], ["sl"], V.tensor_tensor_scan, T.sl[0:C, :], T.nl[0:C, :], T.on[0:C, 0:128], 0.0, A.mult, A.add)
+        op("v", ["sl"], [name], V.tensor_scalar, T[name][0:C, 0:1], T.sl[0:C, 127:128], -1.0, 128.0, A.mult, A.add)
+
+    scores("ur", "urs", ["ur", "urs"], "ta", "tas", ["ta"], 0)
+    first_half("ta", "tas", ["ta"], 0, "ra", "n1", "h1", "qh1", "sh1")
+    op("v", ["p2", "pm0"], ["nb0"], V.tensor_scalar, T.nb[:, 0:128], T.p2[:, 0:128], T.pm0[:, 0:1], None, A.not_equal)
+    op("v", ["p2", "pm1"], ["nb1"], V.tensor_scalar, T.nb[:, 128:256], T.p2[:, 0:128], T.pm1[:, 0:1], None, A.not_equal)
+    op("v", ["nb0", "nb1", "on"], ["sc"], V.tensor_tensor_scan, T.sc[:], T.nb[:], T.on[:], 0.0, A.mult, A.add)
+    op("v", ["sc"], ["lst"], V.tensor_scalar, T.lst[:], T.sc[:, 127:256:128], -1.0, 128.0, A.mult, A.add)
+    second_half("ra", "n1", "qn", "sn", "qn")
+    op("v", ["qn", "lst"], ["pk"], V.tensor_copy, word("pk", 0, 32), word("qn", 0, 128).indirect(T.lst[:, 0:2]))
+    op("s", ["qn", "lst"], ["pks"], S.activation, T.pks[:, 0:32], T.sn[:, 0:128].indirect(T.lst[:, 0:2]), F.Copy)
+    send(["pk"], nxt, code("tb", 128, 160), code("pk", 0, 32), "arrn")
+    send(["pks"], nxt, T.tbs[:, 128:160], T.pks[:, 0:32], "arrn")
+
+    scores("up", "ups", ["up", "ups"], "tb", "tbs", ["tb"], 0)
+    compare("h1", "qh2", "sh2")
+    ranks("qh2", "sh2")
+    op("v", ["jm", "pm0"], ["km"], V.tensor_scalar, T.km[:], T.jm[:], T.pm0[:, 0:1], 256.0, A.not_equal, A.mult)
+    op("v", ["jm"], ["cr"], V.tensor_scalar, T.cr[:], T.jm[:], 0.0, 256.0, A.is_equal, A.mult)
+    op("v", ["j16", "pm0"], ["j8"], V.tensor_scalar, T.j8[:], T.j16[:], T.pm0[:, 0:1], None, A.add)
+    op("v", ["j8"], ["jr"], V.tensor_scalar, T.jr[:], T.j8[:], -1.0, 128.0, A.mult, A.add)
+    op("v", ["p2", "km"], ["mk"], V.tensor_tensor, T.mk[:], T.p2[:, 0:128], T.km[:], A.max)
+    op("v", ["cr", "mk"], ["r8"], V.tensor_tensor_scan, T.r8[:], T.cr[:], T.mk[:], 256.0, A.max, A.min)
+    op("v", ["r8"], ["c8"], V.tensor_scalar, T.c8[:], T.r8[:, 15:128:16], float(C), None, A.is_lt)
+    op("v", ["r8", "jr"], ["d8"], V.tensor_tensor, T.d8[:], T.r8[:, 15:128:16], T.jr[:], A.add)
+    op("v", ["c8", "d8"], ["e8"], V.tensor_tensor, T.e8[:], T.c8[:], T.d8[:], A.mult)
+    op("v", ["e8", "j8"], ["f8"], V.tensor_tensor, T.f8[:], T.e8[:], T.j8[:], A.add)
+    op("v", ["f8"], ["off1"], V.tensor_copy, T.off1[:], T.f8[:])
+    places("li0")
+    dma("y", "dl0", ["li0"], [], T.li[0:1, 0:C], T.li0[0:C, 0:1])
+    op("v", ["gs", "pm0"], ["ca"], V.tensor_scalar, T.ca[:], T.gs[:], T.pm0[:, 0:1], 1.0 / 128, A.add, A.mult)
+    op("g", ["ca"], ["cb"], g.affine_select, T.cb[:], T.ca[:], [[0, 8], [1, 16]], A.is_equal, -1.0, 0, 0)
+    op("v", ["jm", "pm0"], ["thr"], V.tensor_scalar, T.thr[:], T.jm[:], T.pm0[:, 0:1], float(C), A.is_equal, A.mult)
+    op("v", [], ["h3"], V.memset, T.h3[:], 0.0)
+    op("v", ["w"], ["qw"], V.quantize_mx, T.qw[:], T.sw[:], T.wb[:])
+
+    op("v", ["tb", "tn", "off1"], ["t1"], V.tensor_copy, word("win", 128, 256), word("tb", 0, 160).indirect(T.off1[:, 0:8]))
+    op("s", ["tb", "tn", "off1"], ["t1s"], S.activation, T.wins[:, 128:256], T.tbs[:, 0:160].indirect(T.off1[:, 0:8]), F.Copy)
+    tk = ["t1", "t1s"]
+    scores("ur", "urs", ["ur", "urs"], "win", "wins", tk, 128)
+    first_half("win", "wins", tk, 128, "rb", "n2", "h3", "qh3", "sh3")
+    op("v", ["p2", "thr"], ["fl"], V.tensor_tensor, T.fl[:], T.p2[:, 0:128], T.thr[:], A.is_lt)
+    op("v", ["cb", "fl"], ["st"], V.tensor_tensor_scan, T.st[:], T.cb[:], T.fl[:], 0.0, A.max, A.subtract)
+    op("v", ["st"], ["off2"], V.tensor_scalar, T.off2[:], T.st[:, 15:128:16], 128.0, None, A.mult)
+    second_half("rb", "n2", "win", "wins", "n2q")
+    op("v", tk + ["n2q", "off2"], ["t2"], V.tensor_copy, word("t2", 0, 128), word("win", 0, 256).indirect(T.off2[:, 0:8]))
+    op("s", tk + ["n2q", "off2"], ["t2s"], S.activation, T.t2s[:, 0:128], T.wins[:, 0:256].indirect(T.off2[:, 0:8]), F.Copy)
+
+    mm(["qw", "t2", "t2s"], "p4", "qw", "sw", 0, "t2", "t2s", 0)
+    op("s", ["p4"], ["ys"], S.activation, T.ys[:], T.p4[:, 0:128], F.Copy)
+    places("li1")
+    dma("y", "do", ["t2"], [], T.oc[:, 0:512], code("t2", 0, 128))
+    for k in range(4):
+        dma("y", "ds%d" % k, ["t2s"], [], T.osc[4 * k:4 * k + 4, 0:128], T.t2s[32 * k:32 * k + 4, 0:128])
+    dma("s", "dy", ["ys"], [], T.y[:, 0:128], T.ys[:])
+    dma("y", "dl1", ["li1"], [], T.li[1:2, 0:C], T.li1[0:C, 0:1])
+
+    for q in ("v", "s", "t", "g"):
+        g.wait_ge(T.sem[counter[q]], count[q])
+    for s in LOADS + STORES:
+        g.wait_ge(T.sem[s], 16)
+    g.wait_ge(T.sem.sent, sent)

@@ -6,52 +6,37 @@ C = 32
 FACTOR = 13421773 * 2.0 ** -28
 FAR = 1.0e29
 
-CODE = "float8_e4m3fn_x4"
-SCRATCH = {
-    "xb": ("sbuf", [128, 512], "bfloat16"), "ub": ("sbuf", [128, 512], "bfloat16"),
-    "vb": ("sbuf", [128, 2048], "bfloat16"), "wb": ("sbuf", [128, 512], "bfloat16"),
-    "zf": ("sbuf", [128, 128], "float32"), "ob": ("sbuf", [128, 128], "bfloat16"),
-    "idn": ("sbuf", [128, 128], "bfloat16"), "eb": ("sbuf", [128, 520], "bfloat16"),
-    "wo": ("sbuf", [128, 512], "bfloat16"), "later": ("sbuf", [128, 128], "float32"),
-    "jm": ("sbuf", [128, 128], "float32"), "gs": ("sbuf", [128, 128], "float32"),
-    "pif": ("sbuf", [128, 1], "float32"), "pii": ("sbuf", [128, 1], "int32"), "pmi": ("sbuf", [128, 1], "int32"),
-    "pm0": ("sbuf", [128, 1], "float32"), "pm1": ("sbuf", [128, 1], "float32"),
-    "thr": ("sbuf", [128, 128], "bfloat16"), "km": ("sbuf", [128, 128], "bfloat16"),
-    "cr": ("sbuf", [128, 128], "bfloat16"), "ca": ("sbuf", [128, 128], "bfloat16"), "cb": ("sbuf", [128, 128], "bfloat16"),
-    "on": ("sbuf", [128, 256], "bfloat16"), "z8": ("sbuf", [128, 8], "uint16"),
-    "j16": ("sbuf", [128, 8], "float32"), "j8": ("sbuf", [128, 8], "float32"), "jr": ("sbuf", [128, 8], "float32"),
-    "qx": ("sbuf", [128, 128], CODE), "sx": ("sbuf", [128, 128], "uint8"),
-    "qu": ("sbuf", [128, 128], CODE), "su": ("sbuf", [128, 128], "uint8"),
-    "qv": ("sbuf", [128, 512], CODE), "sv": ("sbuf", [128, 512], "uint8"),
-    "qw": ("sbuf", [128, 128], CODE), "sw": ("sbuf", [128, 128], "uint8"),
-    "qe": ("sbuf", [128, 512], CODE), "se": ("sbuf", [128, 512], "uint8"),
-    "qo": ("sbuf", [128, 128], CODE), "so": ("sbuf", [128, 128], "uint8"),
-    "ur": ("sbuf", [128, 128], CODE), "urs": ("sbuf", [128, 128], "uint8"),
-    "up": ("sbuf", [128, 128], CODE), "ups": ("sbuf", [128, 128], "uint8"),
-    "tu": ("sbuf", [128, 8], CODE), "tus": ("sbuf", [128, 32], "uint8"),
-    "ta": ("sbuf", [128, 128], CODE), "tas": ("sbuf", [128, 128], "uint8"),
-    "tb": ("sbuf", [128, 160], CODE), "tbs": ("sbuf", [128, 160], "uint8"),
-    "sm": ("sbuf", [128, 128], "float32"),
-    "h1": ("sbuf", [128, 512], "bfloat16"), "h3": ("sbuf", [128, 512], "bfloat16"),
-    "qh1": ("sbuf", [128, 128], CODE), "sh1": ("sbuf", [128, 128], "uint8"),
-    "qh2": ("sbuf", [128, 128], CODE), "sh2": ("sbuf", [128, 128], "uint8"),
-    "qh3": ("sbuf", [128, 128], CODE), "sh3": ("sbuf", [128, 128], "uint8"),
-    "nb": ("sbuf", [128, 256], "bfloat16"), "sc": ("sbuf", [128, 256], "bfloat16"),
-    "lst": ("sbuf", [128, 2], "uint16"),
-    "mk": ("sbuf", [128, 128], "bfloat16"), "r8": ("sbuf", [128, 128], "bfloat16"),
-    "c8": ("sbuf", [128, 8], "float32"), "d8": ("sbuf", [128, 8], "float32"), "e8": ("sbuf", [128, 8], "float32"),
-    "f8": ("sbuf", [128, 8], "float32"), "off1": ("sbuf", [128, 8], "uint16"),
-    "fl": ("sbuf", [128, 128], "bfloat16"), "st": ("sbuf", [128, 128], "bfloat16"), "off2": ("sbuf", [128, 8], "uint16"),
-    "nl": ("sbuf", [128, 128], "bfloat16"), "sl": ("sbuf", [128, 128], "bfloat16"),
-    "li0": ("sbuf", [128, 1], "float32"), "li1": ("sbuf", [128, 1], "float32"),
-    "ra": ("sbuf", [128, 512], "float32"), "rb": ("sbuf", [128, 512], "float32"),
-    "n1": ("sbuf", [128, 512], "bfloat16"), "n2": ("sbuf", [128, 512], "bfloat16"),
-    "qn": ("sbuf", [128, 128], CODE), "sn": ("sbuf", [128, 128], "uint8"),
-    "pk": ("sbuf", [128, 32], CODE), "pks": ("sbuf", [128, 32], "uint8"),
-    "win": ("sbuf", [128, 256], CODE), "wins": ("sbuf", [128, 256], "uint8"),
-    "t2": ("sbuf", [128, 128], CODE), "t2s": ("sbuf", [128, 128], "uint8"),
-    "ys": ("sbuf", [128, 128], "float32"),
-}
+SCRATCH = {}
+
+
+def _declare(kind, width, *names):
+    for n in names:
+        SCRATCH[n] = ("sbuf", [128, width], kind)
+
+
+def _pair(width, *names):
+    for n in names:
+        _declare("float8_e4m3fn_x4", width, n)
+        _declare("uint8", width, n + "s")
+
+
+_declare("bfloat16", 512, "xb", "ub", "wb", "wo", "h1", "n1", "n2")
+_declare("bfloat16", 2048, "vb")
+_declare("bfloat16", 520, "eb")
+_declare("bfloat16", 128, "ob", "idn", "thr", "km", "cr", "ca", "cb", "mk", "r8", "fl", "st", "nl", "sl")
+_declare("bfloat16", 256, "on", "nb", "sc")
+_declare("float32", 128, "zf", "later", "jm", "gs", "sm", "ys")
+_declare("float32", 512, "ra", "rb")
+_declare("float32", 8, "j16", "j8", "jr", "c8", "d8", "e8", "f8")
+_declare("float32", 1, "pif", "pm0", "pm1", "li0", "li1")
+_declare("int32", 1, "pii", "pmi")
+_declare("uint16", 8, "z8", "off1", "off2")
+_declare("uint16", 2, "lst")
+_pair(512, "qv", "qe")
+_pair(256, "win")
+_pair(160, "tb")
+_pair(128, "qx", "qu", "qw", "qo", "ur", "up", "ta", "qh1", "qh2", "qh3", "qn", "t2")
+_pair(32, "tu", "pk")
 for _i in range(8):
     SCRATCH["p%d" % _i] = ("psum", [128, 512], "float32")
 
@@ -105,28 +90,26 @@ def rank_program(g, core, T, topo):
 
     V, S, E = g.vector, g.scalar, g.tensor
     nxt, nxt2 = T.cores[(rank + 1) % N], T.cores[(rank + 2) % N]
+    prv, prv2 = T.cores[(rank - 1) % N], T.cores[(rank - 2) % N]
 
-    def lanes(dst):
-        return topo.engines(core, dst)[:8]
+    def lanes(src, dst):
+        return topo.engines(src, dst)[:8]
 
     def bits(es):
         return sum(1 << e for e in es)
 
+    sent = [0]
+
     def send(reads, dst, out, in_, sem):
         ready("g", reads, [])
         rid, pid = topo.addr(dst, core)
+        es = lanes(core, dst)
+        sent[0] += len(es)
         g.remote_dma(out_ap=out, in_ap=in_, remote_sem=T.sem[sem], local_sem=T.sem.sent, pid=pid, routing_id=rid,
-                     dma_engine_mask=bits(lanes(dst)))
+                     dma_engine_mask=bits(es))
 
-    def lane_count(src, dst):
-        return len(topo.engines(src, dst)[:8])
-
-    me = core
-    prv, prv2 = T.cores[(rank - 1) % N], T.cores[(rank - 2) % N]
-    land = {"tu": ("arru", lane_count(prv, me)), "ta": ("arra", 2 * lane_count(prv, me)),
-            "tb": ("arrb", 2 * lane_count(prv2, me)), "tn": ("arrn", 2 * lane_count(prv, me))}
-    for k, (s, n) in land.items():
-        wrote[k] = (0, s, n, {})
+    for key, sem, src, calls in (("tu", "arru", prv, 1), ("ta", "arra", prv, 2), ("tb", "arrb", prv2, 2), ("tn", "arrn", prv, 2)):
+        wrote[key] = (0, sem, calls * len(lanes(src, core)), {})
 
     def code(name, a, b):
         return T[name][:, a:b].bitcast(dt.uint8)
@@ -134,85 +117,95 @@ def rank_program(g, core, T, topo):
     def word(name, a, b):
         return T[name][:, a:b].bitcast(dt.uint32)
 
+    def quant(key, reads, name, a, in_):
+        op("v", reads, [key], V.quantize_mx, T[name][:, a:a + 128], T[name + "s"][:, a:a + 128], in_)
+
+    def pick(key, reads, dst, n, at, src, a, b, off):
+        op("v", reads, [key], V.tensor_copy, word(dst, at, at + n), word(src, a, b).indirect(off))
+        op("s", reads, [key + "s"], S.activation, T[dst + "s"][:, at:at + n], T[src + "s"][:, a:b].indirect(off), F.Copy)
+
     dma("s", "du", [], ["u"], T.ub[:, 0:8], T.u[:, 0:8])
     dma("y", "dx", [], ["x"], T.xb[:], T.x[:, 0:512])
     dma("y", "dv0", [], ["v0"], T.vb[:, 0:1024], T.v[:, 0:1024])
     dma("y", "dv1", [], ["v1"], T.vb[:, 1024:2048], T.v[:, 1024:2048])
-    dma("s", "dw", [], ["w"], T.wb[:], T.w[:, 0:512])
 
+    small = dict(allow_small_or_imprecise_dtypes=True)
     op("v", [], ["ob"], V.memset, T.ob[:], 1.0)
     op("v", [], ["zf"], V.memset, T.zf[:], 0.0)
     op("g", ["ob"], ["idn"], g.affine_select, T.idn[:], T.ob[:], [[-1, 128]], A.is_equal, 0.0, 0, 1)
     op("g", ["zf"], ["later"], g.affine_select, T.later[:], T.zf[:], [[1, 128]], A.is_gt, FAR, 0, -1)
     op("g", [], ["pii"], g.iota, T.pii[:], [[0, 1]], 0, 1)
-    op("g", [], ["pif"], g.iota, T.pif[:], [[0, 1]], 0, 1, allow_small_or_imprecise_dtypes=True)
-    op("g", [], ["jm"], g.iota, T.jm[:], [[0, 8], [1, 16]], 0, 0, allow_small_or_imprecise_dtypes=True)
-    op("g", [], ["j16"], g.iota, T.j16[:], [[16, 8]], 0, 0, allow_small_or_imprecise_dtypes=True)
+    op("g", [], ["jm"], g.iota, T.jm[:], [[0, 8], [1, 16]], 0, 0, **small)
+    op("g", [], ["j16"], g.iota, T.j16[:], [[16, 8]], 0, 0, **small)
     op("v", [], ["uz"], V.memset, T.ub[:, 8:512], 0.0)
     op("v", [], ["eb"], V.memset, T.eb[:], 0.0)
     op("v", ["idn"], ["eb"], V.tensor_copy, T.eb[:, 3:515:4], T.idn[:])
     for b in range(4):
-        op("v", ["eb"], ["qe%d" % b], V.quantize_mx, T.qe[:, 128 * b:128 * b + 128], T.se[:, 128 * b:128 * b + 128],
-           T.eb[:, 3 - b:515 - b])
+        quant("qe%d" % b, ["eb"], "qe", 128 * b, T.eb[:, 3 - b:515 - b])
     op("v", [], ["z8"], V.memset, T.z8[:], 0)
     op("v", [], ["h1"], V.memset, T.h1[:], 0.0)
 
-    op("v", ["u", "uz"], ["qu"], V.quantize_mx, T.qu[:], T.su[:], T.ub[:])
-    op("v", ["x"], ["qx"], V.quantize_mx, T.qx[:], T.sx[:], T.xb[:])
+    quant("qu", ["u", "uz"], "qu", 0, T.ub[:])
+    quant("qx", ["x"], "qx", 0, T.xb[:])
     ready("g", ["qu"], [])
     rid, pid = topo.addr(nxt, core)
-    es = lanes(nxt)
+    es = lanes(core, nxt)
     half = len(es) // 2
+    sent[0] += len(es)
     to = [DstId(rid=rid, pnc=pid)]
     g.remote_dma_fused([
         RemoteDMATransfer(dst_ids=to, dma_engine_mask=bits(es[:half]), remote_sem=T.sem.arru, src=code("qu", 0, 1), dst=code("tu", 0, 1)),
-        RemoteDMATransfer(dst_ids=to, dma_engine_mask=bits(es[half:]), remote_sem=T.sem.arru, src=T.su[:, 0:4], dst=T.tus[:, 0:4]),
+        RemoteDMATransfer(dst_ids=to, dma_engine_mask=bits(es[half:]), remote_sem=T.sem.arru, src=T.qus[:, 0:4], dst=T.tus[:, 0:4]),
     ], local_sem=T.sem.sent)
     send(["qx"], nxt, code("ta", 0, 128), code("qx", 0, 128), "arra")
-    send(["qx"], nxt, T.tas[:, 0:128], T.sx[:, 0:128], "arra")
+    send(["qx"], nxt, T.tas[:, 0:128], T.qxs[:, 0:128], "arra")
     send(["qx"], nxt2, code("tb", 0, 128), code("qx", 0, 128), "arrb")
-    send(["qx"], nxt2, T.tbs[:, 0:128], T.sx[:, 0:128], "arrb")
-    sent = len(es) + 2 * len(es) + 2 * len(lanes(nxt2)) + 2 * len(es)
+    send(["qx"], nxt2, T.tbs[:, 0:128], T.qxs[:, 0:128], "arrb")
+    op("g", [], ["gs"], g.iota, T.gs[:], [[16, 8], [0, 16]], 128, 0, **small)
+    op("g", [], ["pif"], g.iota, T.pif[:], [[0, 1]], 0, 1, **small)
+    dma("y", "dw", ["ta"], ["w"], T.wb[:], T.w[:, 0:512])
 
-    def repeat(src, srcs, dst, dsts, key, out):
-        op("v", [key, "z8"], [out], V.tensor_copy, word(dst, 0, 128), word(src, 0, 1).indirect(T.z8[:, 0:8]))
-        op("s", [key, "z8"], [out + "s"], S.activation, T[dsts][:, 0:128], T[srcs][:, 0:1].indirect(T.z8[:, 0:8]), F.Copy)
-
-    repeat("qu", "su", "ur", "urs", "qu", "ur")
-    op("v", ["pii"], ["pmi"], V.tensor_scalar, T.pmi[:], T.pii[:], 15, None, A.bitwise_and)
+    pick("ur", ["qu", "z8"], "ur", 128, 0, "qu", 0, 1, T.z8[:, 0:8])
     op("v", [], ["wo"], V.memset, T.wo[:], 1.0)
+    op("v", ["pii"], ["pmi"], V.tensor_scalar, T.pmi[:], T.pii[:], 15, None, A.bitwise_and)
     op("v", [], ["on"], V.memset, T.on[:], 1.0)
+    quant("qo", ["wo"], "qo", 0, T.wo[:])
     op("v", ["pmi"], ["pm0"], V.tensor_copy, T.pm0[:], T.pmi[:])
-    op("v", ["wo"], ["qo"], V.quantize_mx, T.qo[:], T.so[:], T.wo[:])
+    for i in range(2):
+        quant("qv%d" % i, ["v0"], "qv", 128 * i, T.vb[:, 512 * i:512 * i + 512])
     op("v", ["pm0"], ["pm1"], V.tensor_scalar, T.pm1[:], T.pm0[:], 16.0, None, A.add)
-    for i in range(4):
-        op("v", ["v%d" % (i // 2)], ["qv%d" % i], V.quantize_mx, T.qv[:, 128 * i:128 * i + 128], T.sv[:, 128 * i:128 * i + 128],
-           T.vb[:, 512 * i:512 * i + 512])
-    repeat("tu", "tus", "up", "ups", "tu", "up")
-    op("g", [], ["gs"], g.iota, T.gs[:], [[16, 8], [0, 16]], 128, 0, allow_small_or_imprecise_dtypes=True)
+    op("v", ["jm"], ["cr"], V.tensor_scalar, T.cr[:], T.jm[:], 0.0, 256.0, A.is_equal, A.mult)
+    op("v", ["j16", "pm0"], ["j8"], V.tensor_scalar, T.j8[:], T.j16[:], T.pm0[:, 0:1], None, A.add)
+    op("v", ["jm", "pm0"], ["km"], V.tensor_scalar, T.km[:], T.jm[:], T.pm0[:, 0:1], 256.0, A.not_equal, A.mult)
+    op("v", ["j8"], ["jr"], V.tensor_scalar, T.jr[:], T.j8[:], -1.0, 128.0, A.mult, A.add)
+    for i in range(2, 4):
+        quant("qv%d" % i, ["v1"], "qv", 128 * i, T.vb[:, 512 * i:512 * i + 512])
+    op("v", ["gs", "pm0"], ["ca"], V.tensor_scalar, T.ca[:], T.gs[:], T.pm0[:, 0:1], 1.0 / 128, A.add, A.mult)
+    op("g", ["ca"], ["cb"], g.affine_select, T.cb[:], T.ca[:], [[0, 8], [1, 16]], A.is_equal, -1.0, 0, 0)
+    pick("up", ["tu", "z8"], "up", 128, 0, "tu", 0, 1, T.z8[:, 0:8])
 
-    def mm(reads, bank, w, ws, a, x, xs, b, n=128):
-        op("t", reads, [bank], E.matmul_mx, T[bank][:, 0:n], T[w][:, a:a + 128], T[ws][:, a:a + 128],
-           T[x][:, b:b + n], T[xs][:, b:b + n], True, True)
+    def mm(reads, bank, w, a, x, b):
+        op("t", reads, [bank], E.matmul_mx, T[bank][:, 0:128], T[w][:, a:a + 128], T[w + "s"][:, a:a + 128],
+           T[x][:, b:b + 128], T[x + "s"][:, b:b + 128], True, True)
 
-    def scores(u, us, ukeys, t, ts, tk, at):
-        mm(ukeys + tk, "p0", t, ts, at, u, us, 0)
-        mm(ukeys + tk, "p1", u, us, 0, t, ts, at)
+    def scores(u, t, tk, at=0):
+        mm([u, u + "s"] + tk, "p0", t, at, u, 0)
+        mm([u, u + "s"] + tk, "p1", u, 0, t, at)
 
-    def compare(h, qh, sh):
+    def compare(qh):
         op("v", ["later", "p0"], ["sm"], V.tensor_scalar, T.sm[:], T.later[:], T.p0[:, 0:1], None, A.add)
-        op("v", ["p0", "p1"], [h], V.tensor_scalar, T[h][:, 0:512:4], T.p1[:, 0:128], T.p0[:, 0:1], None, A.is_lt)
-        op("v", ["sm", "p1"], [h + "e"], V.tensor_tensor, T[h][:, 1:512:4], T.p1[:, 0:128], T.sm[:], A.is_equal)
-        op("v", [h, h + "e"], [qh], V.quantize_mx, T[qh][:], T[sh][:], T[h][:])
+        op("v", ["p0", "p1"], ["h1"], V.tensor_scalar, T.h1[:, 0:512:4], T.p1[:, 0:128], T.p0[:, 0:1], None, A.is_lt)
+        op("v", ["sm", "p1"], ["h1e"], V.tensor_tensor, T.h1[:, 1:512:4], T.p1[:, 0:128], T.sm[:], A.is_equal)
+        quant(qh, ["h1", "h1e"], qh, 0, T.h1[:])
 
-    def ranks(qh, sh):
-        mm(["qo", qh], "p2", "qo", "so", 0, qh, sh, 0)
+    def ranks(qh, bank):
+        mm(["qo", qh], bank, "qo", 0, qh, 0)
 
-    def row(i, bank, t, ts, tk, at):
-        mm(["qv%d" % i] + tk, bank, "qv", "sv", 128 * i, t, ts, at)
+    def row(i, bank, t, tk, at):
+        mm(["qv%d" % i] + tk, bank, "qv", 128 * i, t, at)
 
-    def old(i, bank, t, ts, tk, at):
-        mm(["qe%d" % i] + tk, bank, "qe", "se", 128 * i, t, ts, at)
+    def old(i, bank, t, tk, at):
+        mm(["qe%d" % i] + tk, bank, "qe", 128 * i, t, at)
 
     def relu(i, bank, r):
         op("s", [bank], [r + str(i)], S.activation, T[r][:, 128 * i:128 * i + 128], T[bank][:, 0:128], F.Relu, scale=FACTOR)
@@ -221,52 +214,45 @@ def rank_program(g, core, T, topo):
         op("v", [bank, r + str(i)], [n + str(i)], V.tensor_tensor, T[n][:, i:512:4], T[bank][:, 0:128],
            T[r][:, 128 * i:128 * i + 128], A.add)
 
-    def first_half(t, ts, tk, at, r, n, h, qh, sh):
-        row(0, "p3", t, ts, tk, at)
-        row(1, "p4", t, ts, tk, at)
-        old(0, "p5", t, ts, tk, at)
-        old(1, "p6", t, ts, tk, at)
-        row(2, "p7", t, ts, tk, at)
-        compare(h, qh, sh)
-        ranks(qh, sh)
-        for i, b in enumerate(["p3", "p4", "p7"]):
-            relu(i, b, r)
-        add(0, "p5", r, n)
-        add(1, "p6", r, n)
-        row(3, "p3", t, ts, tk, at)
-        old(2, "p5", t, ts, tk, at)
-        old(3, "p6", t, ts, tk, at)
-        relu(3, "p3", r)
-
-    def second_half(r, n, q, s, key):
-        add(2, "p5", r, n)
-        add(3, "p6", r, n)
-        op("v", [n + str(i) for i in range(4)], [key], V.quantize_mx, T[q][:, 0:128], T[s][:, 0:128], T[n][:])
-
     def places(name):
         op("v", ["p2", "pif"], ["nl"], V.tensor_scalar, T.nl[0:C, :], T.p2[0:C, 0:128], T.pif[0:C, 0:1], None, A.not_equal)
         op("v", ["nl", "on"], ["sl"], V.tensor_tensor_scan, T.sl[0:C, :], T.nl[0:C, :], T.on[0:C, 0:128], 0.0, A.mult, A.add)
         op("v", ["sl"], [name], V.tensor_scalar, T[name][0:C, 0:1], T.sl[0:C, 127:128], -1.0, 128.0, A.mult, A.add)
 
-    scores("ur", "urs", ["ur", "urs"], "ta", "tas", ["ta"], 0)
-    first_half("ta", "tas", ["ta"], 0, "ra", "n1", "h1", "qh1", "sh1")
+    def first_half(t, tk, at, r, n, qh):
+        row(0, "p3", t, tk, at)
+        row(1, "p4", t, tk, at)
+        old(0, "p5", t, tk, at)
+        old(1, "p6", t, tk, at)
+        row(2, "p7", t, tk, at)
+        compare(qh)
+        ranks(qh, "p2")
+        for i, b in enumerate(["p3", "p4", "p7"]):
+            relu(i, b, r)
+        row(3, "p0", t, tk, at)
+        old(2, "p3", t, tk, at)
+        old(3, "p4", t, tk, at)
+        relu(3, "p0", r)
+        add(0, "p5", r, n)
+        add(1, "p6", r, n)
+
+    scores("ur", "ta", ["ta"])
+    first_half("ta", ["ta"], 0, "ra", "n1", "qh1")
     op("v", ["p2", "pm0"], ["nb0"], V.tensor_scalar, T.nb[:, 0:128], T.p2[:, 0:128], T.pm0[:, 0:1], None, A.not_equal)
     op("v", ["p2", "pm1"], ["nb1"], V.tensor_scalar, T.nb[:, 128:256], T.p2[:, 0:128], T.pm1[:, 0:1], None, A.not_equal)
+    add(2, "p3", "ra", "n1")
     op("v", ["nb0", "nb1", "on"], ["sc"], V.tensor_tensor_scan, T.sc[:], T.nb[:], T.on[:], 0.0, A.mult, A.add)
+    add(3, "p4", "ra", "n1")
     op("v", ["sc"], ["lst"], V.tensor_scalar, T.lst[:], T.sc[:, 127:256:128], -1.0, 128.0, A.mult, A.add)
-    second_half("ra", "n1", "qn", "sn", "qn")
-    op("v", ["qn", "lst"], ["pk"], V.tensor_copy, word("pk", 0, 32), word("qn", 0, 128).indirect(T.lst[:, 0:2]))
-    op("s", ["qn", "lst"], ["pks"], S.activation, T.pks[:, 0:32], T.sn[:, 0:128].indirect(T.lst[:, 0:2]), F.Copy)
+    quant("qn", ["n1%d" % i for i in range(4)], "qn", 0, T.n1[:])
+    pick("pk", ["qn", "lst"], "pk", 32, 0, "qn", 0, 128, T.lst[:, 0:2])
     send(["pk"], nxt, code("tb", 128, 160), code("pk", 0, 32), "arrn")
     send(["pks"], nxt, T.tbs[:, 128:160], T.pks[:, 0:32], "arrn")
 
-    scores("up", "ups", ["up", "ups"], "tb", "tbs", ["tb"], 0)
-    compare("h1", "qh2", "sh2")
-    ranks("qh2", "sh2")
-    op("v", ["jm", "pm0"], ["km"], V.tensor_scalar, T.km[:], T.jm[:], T.pm0[:, 0:1], 256.0, A.not_equal, A.mult)
-    op("v", ["jm"], ["cr"], V.tensor_scalar, T.cr[:], T.jm[:], 0.0, 256.0, A.is_equal, A.mult)
-    op("v", ["j16", "pm0"], ["j8"], V.tensor_scalar, T.j8[:], T.j16[:], T.pm0[:, 0:1], None, A.add)
-    op("v", ["j8"], ["jr"], V.tensor_scalar, T.jr[:], T.j8[:], -1.0, 128.0, A.mult, A.add)
+    scores("up", "tb", ["tb"])
+    compare("qh2")
+    ranks("qh2", "p2")
+    op("v", ["jm", "pm0"], ["thr"], V.tensor_scalar, T.thr[:], T.jm[:], T.pm0[:, 0:1], float(C), A.is_equal, A.mult)
     op("v", ["p2", "km"], ["mk"], V.tensor_tensor, T.mk[:], T.p2[:, 0:128], T.km[:], A.max)
     op("v", ["cr", "mk"], ["r8"], V.tensor_tensor_scan, T.r8[:], T.cr[:], T.mk[:], 256.0, A.max, A.min)
     op("v", ["r8"], ["c8"], V.tensor_scalar, T.c8[:], T.r8[:, 15:128:16], float(C), None, A.is_lt)
@@ -274,27 +260,23 @@ def rank_program(g, core, T, topo):
     op("v", ["c8", "d8"], ["e8"], V.tensor_tensor, T.e8[:], T.c8[:], T.d8[:], A.mult)
     op("v", ["e8", "j8"], ["f8"], V.tensor_tensor, T.f8[:], T.e8[:], T.j8[:], A.add)
     op("v", ["f8"], ["off1"], V.tensor_copy, T.off1[:], T.f8[:])
+    quant("qw", ["w"], "qw", 0, T.wb[:])
     places("li0")
     dma("y", "dl0", ["li0"], [], T.li[0:1, 0:C], T.li0[0:C, 0:1])
-    op("v", ["gs", "pm0"], ["ca"], V.tensor_scalar, T.ca[:], T.gs[:], T.pm0[:, 0:1], 1.0 / 128, A.add, A.mult)
-    op("g", ["ca"], ["cb"], g.affine_select, T.cb[:], T.ca[:], [[0, 8], [1, 16]], A.is_equal, -1.0, 0, 0)
-    op("v", ["jm", "pm0"], ["thr"], V.tensor_scalar, T.thr[:], T.jm[:], T.pm0[:, 0:1], float(C), A.is_equal, A.mult)
-    op("v", [], ["h3"], V.memset, T.h3[:], 0.0)
-    op("v", ["w"], ["qw"], V.quantize_mx, T.qw[:], T.sw[:], T.wb[:])
 
-    op("v", ["tb", "tn", "off1"], ["t1"], V.tensor_copy, word("win", 128, 256), word("tb", 0, 160).indirect(T.off1[:, 0:8]))
-    op("s", ["tb", "tn", "off1"], ["t1s"], S.activation, T.wins[:, 128:256], T.tbs[:, 0:160].indirect(T.off1[:, 0:8]), F.Copy)
+    pick("t1", ["tb", "tn", "off1"], "win", 128, 128, "tb", 0, 160, T.off1[:, 0:8])
     tk = ["t1", "t1s"]
-    scores("ur", "urs", ["ur", "urs"], "win", "wins", tk, 128)
-    first_half("win", "wins", tk, 128, "rb", "n2", "h3", "qh3", "sh3")
+    scores("ur", "win", tk, 128)
+    first_half("win", tk, 128, "rb", "n2", "qh3")
     op("v", ["p2", "thr"], ["fl"], V.tensor_tensor, T.fl[:], T.p2[:, 0:128], T.thr[:], A.is_lt)
+    add(2, "p3", "rb", "n2")
     op("v", ["cb", "fl"], ["st"], V.tensor_tensor_scan, T.st[:], T.cb[:], T.fl[:], 0.0, A.max, A.subtract)
+    add(3, "p4", "rb", "n2")
     op("v", ["st"], ["off2"], V.tensor_scalar, T.off2[:], T.st[:, 15:128:16], 128.0, None, A.mult)
-    second_half("rb", "n2", "win", "wins", "n2q")
-    op("v", tk + ["n2q", "off2"], ["t2"], V.tensor_copy, word("t2", 0, 128), word("win", 0, 256).indirect(T.off2[:, 0:8]))
-    op("s", tk + ["n2q", "off2"], ["t2s"], S.activation, T.t2s[:, 0:128], T.wins[:, 0:256].indirect(T.off2[:, 0:8]), F.Copy)
+    quant("n2q", ["n2%d" % i for i in range(4)], "win", 0, T.n2[:])
+    pick("t2", tk + ["n2q", "off2"], "t2", 128, 0, "win", 0, 256, T.off2[:, 0:8])
 
-    mm(["qw", "t2", "t2s"], "p4", "qw", "sw", 0, "t2", "t2s", 0)
+    mm(["qw", "t2", "t2s"], "p4", "qw", 0, "t2", 0)
     op("s", ["p4"], ["ys"], S.activation, T.ys[:], T.p4[:, 0:128], F.Copy)
     places("li1")
     dma("y", "do", ["t2"], [], T.oc[:, 0:512], code("t2", 0, 128))
@@ -307,4 +289,4 @@ def rank_program(g, core, T, topo):
         g.wait_ge(T.sem[counter[q]], count[q])
     for s in LOADS + STORES:
         g.wait_ge(T.sem[s], 16)
-    g.wait_ge(T.sem.sent, sent)
+    g.wait_ge(T.sem.sent, sent[0])

@@ -1,4 +1,3 @@
-from concourse.bass import DstId, RemoteDMATransfer
 from concourse.mybir import dt, AluOpType, ActivationFunctionType
 
 N = 8
@@ -20,14 +19,13 @@ def _pair(width, *names):
         _declare("uint8", width, n + "s")
 
 
-_declare("bfloat16", 512, "xb", "ub", "wb", "wo", "h1", "n1", "n2")
+_declare("bfloat16", 512, "xb", "ub", "wb", "wo", "wp", "h1", "n1", "n2")
 _declare("bfloat16", 2048, "vb")
 _declare("bfloat16", 520, "eb")
-_declare("bfloat16", 128, "ob", "idn", "thr", "km", "cr", "ca", "cb", "mk", "r8", "fl", "st", "nl", "sl")
+_declare("bfloat16", 128, "ob", "idn", "thr", "cr", "cx", "ca", "cb", "mk", "ml", "r8", "fl", "st", "nl", "sl")
 _declare("bfloat16", 256, "on", "nb", "sc")
 _declare("float32", 128, "zf", "later", "jm", "gs", "sm", "ys")
 _declare("float32", 512, "ra", "rb")
-_declare("float32", 8, "j16", "j8", "jr", "c8", "d8", "e8", "f8")
 _declare("float32", 1, "pif", "pm0", "pm1", "li0", "li1")
 _declare("int32", 1, "pii", "pmi")
 _declare("uint16", 8, "z8", "off1", "off2")
@@ -35,14 +33,14 @@ _declare("uint16", 2, "lst")
 _pair(512, "qv", "qe")
 _pair(256, "win")
 _pair(160, "tb")
-_pair(128, "qx", "qu", "qw", "qo", "ur", "up", "ta", "qh1", "qh2", "qh3", "qn", "t2")
+_pair(128, "qx", "qu", "qw", "qo", "qk", "ur", "up", "ta", "qh1", "qh2", "qh3", "qn", "t2")
 _pair(32, "tu", "pk")
 for _i in range(8):
     SCRATCH["p%d" % _i] = ("psum", [128, 512], "float32")
 
 LOADS = ["dx", "du", "dv0", "dv1", "dw"]
 STORES = ["do", "ds0", "ds1", "ds2", "ds3", "dy", "dl0", "dl1"]
-SEMAPHORES = ["cv", "cs", "ct", "cg", "sent", "arru", "arra", "arrb", "arrn"] + LOADS + STORES
+SEMAPHORES = ["cv", "cs", "ct", "cg", "sent", "arru", "arrs", "arra", "arrb", "arrn"] + LOADS + STORES
 
 
 def rank_program(g, core, T, topo):
@@ -95,9 +93,6 @@ def rank_program(g, core, T, topo):
     def lanes(src, dst):
         return topo.engines(src, dst)[:8]
 
-    def bits(es):
-        return sum(1 << e for e in es)
-
     sent = [0]
 
     def send(reads, dst, out, in_, sem):
@@ -106,83 +101,87 @@ def rank_program(g, core, T, topo):
         es = lanes(core, dst)
         sent[0] += len(es)
         g.remote_dma(out_ap=out, in_ap=in_, remote_sem=T.sem[sem], local_sem=T.sem.sent, pid=pid, routing_id=rid,
-                     dma_engine_mask=bits(es))
+                     dma_engine_mask=sum(1 << e for e in es))
 
-    for key, sem, src, calls in (("tu", "arru", prv, 1), ("ta", "arra", prv, 2), ("tb", "arrb", prv2, 2), ("tn", "arrn", prv, 2)):
+    for key, sem, src, calls in (("tu", "arru", prv, 1), ("tus", "arrs", prv, 1), ("ta", "arra", prv, 2),
+                                 ("tb", "arrb", prv2, 2), ("tn", "arrn", prv, 2)):
         wrote[key] = (0, sem, calls * len(lanes(src, core)), {})
 
     def code(name, a, b):
         return T[name][:, a:b].bitcast(dt.uint8)
 
-    def word(name, a, b):
-        return T[name][:, a:b].bitcast(dt.uint32)
-
     def quant(key, reads, name, a, in_):
         op("v", reads, [key], V.quantize_mx, T[name][:, a:a + 128], T[name + "s"][:, a:a + 128], in_)
 
-    def pick(key, reads, dst, n, at, src, a, b, off):
-        op("v", reads, [key], V.tensor_copy, word(dst, at, at + n), word(src, a, b).indirect(off))
+    def pick_codes(key, reads, dst, n, at, src, a, b, off):
+        op("v", reads, [key], V.tensor_copy, T[dst][:, at:at + n].bitcast(dt.uint32), T[src][:, a:b].bitcast(dt.uint32).indirect(off))
+
+    def pick_scales(key, reads, dst, n, at, src, a, b, off):
         op("s", reads, [key + "s"], S.activation, T[dst + "s"][:, at:at + n], T[src + "s"][:, a:b].indirect(off), F.Copy)
+
+    def pick(*args):
+        pick_codes(*args)
+        pick_scales(*args)
 
     dma("s", "du", [], ["u"], T.ub[:, 0:8], T.u[:, 0:8])
     dma("y", "dx", [], ["x"], T.xb[:], T.x[:, 0:512])
     dma("y", "dv0", [], ["v0"], T.vb[:, 0:1024], T.v[:, 0:1024])
     dma("y", "dv1", [], ["v1"], T.vb[:, 1024:2048], T.v[:, 1024:2048])
+    dma("y", "dw", ["tu"], ["w"], T.wb[:], T.w[:, 0:512])
 
     small = dict(allow_small_or_imprecise_dtypes=True)
     op("v", [], ["ob"], V.memset, T.ob[:], 1.0)
     op("v", [], ["zf"], V.memset, T.zf[:], 0.0)
     op("g", ["ob"], ["idn"], g.affine_select, T.idn[:], T.ob[:], [[-1, 128]], A.is_equal, 0.0, 0, 1)
-    op("g", ["zf"], ["later"], g.affine_select, T.later[:], T.zf[:], [[1, 128]], A.is_gt, FAR, 0, -1)
     op("g", [], ["pii"], g.iota, T.pii[:], [[0, 1]], 0, 1)
     op("g", [], ["jm"], g.iota, T.jm[:], [[0, 8], [1, 16]], 0, 0, **small)
-    op("g", [], ["j16"], g.iota, T.j16[:], [[16, 8]], 0, 0, **small)
-    op("v", [], ["uz"], V.memset, T.ub[:, 8:512], 0.0)
+    op("g", [], ["pif"], g.iota, T.pif[:], [[0, 1]], 0, 1, **small)
+    op("g", [], ["gs"], g.iota, T.gs[:], [[16, 8], [0, 16]], 128, 0, **small)
+    op("g", ["zf"], ["later"], g.affine_select, T.later[:], T.zf[:], [[1, 128]], A.is_gt, FAR, 0, -1)
+
+    def ones(name, width, first=0):
+        keys = [name + str(i) for i in range(width // 128)]
+        for i, k in enumerate(keys):
+            a, b = max(first, 128 * i), 128 * i + 128
+            op("s", ["ob"], [k], S.activation, T[name][:, a:b], T.ob[:, 0:b - a], F.Copy)
+        return keys
+
+    uz = ones("ub", 512, 8)
+    wo, wp, on = ones("wo", 512), ones("wp", 512), ones("on", 256)
     op("v", [], ["eb"], V.memset, T.eb[:], 0.0)
+    op("v", [], ["z8"], V.memset, T.z8[:], 0)
+    op("v", [], ["h1y"], V.memset, T.h1[:, 3:512:4], 0.0)
     op("v", ["idn"], ["eb"], V.tensor_copy, T.eb[:, 3:515:4], T.idn[:])
     for b in range(4):
         quant("qe%d" % b, ["eb"], "qe", 128 * b, T.eb[:, 3 - b:515 - b])
-    op("v", [], ["z8"], V.memset, T.z8[:], 0)
-    op("v", [], ["h1"], V.memset, T.h1[:], 0.0)
+    op("v", ["pii"], ["pmi"], V.tensor_scalar, T.pmi[:], T.pii[:], 15, None, A.bitwise_and)
+    op("v", [], wo, V.memset, T.wo[:, 2:512:4], 0.0)
+    op("v", ["pmi"], ["pm0"], V.tensor_copy, T.pm0[:], T.pmi[:])
+    quant("qo", wo, "qo", 0, T.wo[:])
+    op("v", ["pm0"], ["pm1"], V.tensor_scalar, T.pm1[:], T.pm0[:], 16.0, None, A.add)
 
-    quant("qu", ["u", "uz"], "qu", 0, T.ub[:])
+    quant("qu", ["u"] + uz, "qu", 0, T.ub[:])
     quant("qx", ["x"], "qx", 0, T.xb[:])
-    ready("g", ["qu"], [])
-    rid, pid = topo.addr(nxt, core)
-    es = lanes(core, nxt)
-    half = len(es) // 2
-    sent[0] += len(es)
-    to = [DstId(rid=rid, pnc=pid)]
-    g.remote_dma_fused([
-        RemoteDMATransfer(dst_ids=to, dma_engine_mask=bits(es[:half]), remote_sem=T.sem.arru, src=code("qu", 0, 1), dst=code("tu", 0, 1)),
-        RemoteDMATransfer(dst_ids=to, dma_engine_mask=bits(es[half:]), remote_sem=T.sem.arru, src=T.qus[:, 0:4], dst=T.tus[:, 0:4]),
-    ], local_sem=T.sem.sent)
+    send(["qu"], nxt, code("tu", 0, 1), code("qu", 0, 1), "arru")
     send(["qx"], nxt, code("ta", 0, 128), code("qx", 0, 128), "arra")
     send(["qx"], nxt, T.tas[:, 0:128], T.qxs[:, 0:128], "arra")
-    send(["qx"], nxt2, code("tb", 0, 128), code("qx", 0, 128), "arrb")
-    send(["qx"], nxt2, T.tbs[:, 0:128], T.qxs[:, 0:128], "arrb")
-    op("g", [], ["gs"], g.iota, T.gs[:], [[16, 8], [0, 16]], 128, 0, **small)
-    op("g", [], ["pif"], g.iota, T.pif[:], [[0, 1]], 0, 1, **small)
-    dma("y", "dw", ["ta"], ["w"], T.wb[:], T.w[:, 0:512])
+    send(["qu"], nxt, T.tus[:, 0:2], T.qus[:, 0:2], "arrs")
+    send(["qx"], nxt2, code("tb", C, C + 128), code("qx", 0, 128), "arrb")
+    send(["qx"], nxt2, T.tbs[:, C:C + 128], T.qxs[:, 0:128], "arrb")
 
     pick("ur", ["qu", "z8"], "ur", 128, 0, "qu", 0, 1, T.z8[:, 0:8])
-    op("v", [], ["wo"], V.memset, T.wo[:], 1.0)
-    op("v", ["pii"], ["pmi"], V.tensor_scalar, T.pmi[:], T.pii[:], 15, None, A.bitwise_and)
-    op("v", [], ["on"], V.memset, T.on[:], 1.0)
-    quant("qo", ["wo"], "qo", 0, T.wo[:])
-    op("v", ["pmi"], ["pm0"], V.tensor_copy, T.pm0[:], T.pmi[:])
-    for i in range(2):
-        quant("qv%d" % i, ["v0"], "qv", 128 * i, T.vb[:, 512 * i:512 * i + 512])
-    op("v", ["pm0"], ["pm1"], V.tensor_scalar, T.pm1[:], T.pm0[:], 16.0, None, A.add)
-    op("v", ["jm"], ["cr"], V.tensor_scalar, T.cr[:], T.jm[:], 0.0, 256.0, A.is_equal, A.mult)
-    op("v", ["j16", "pm0"], ["j8"], V.tensor_scalar, T.j8[:], T.j16[:], T.pm0[:, 0:1], None, A.add)
-    op("v", ["jm", "pm0"], ["km"], V.tensor_scalar, T.km[:], T.jm[:], T.pm0[:, 0:1], 256.0, A.not_equal, A.mult)
-    op("v", ["j8"], ["jr"], V.tensor_scalar, T.jr[:], T.j8[:], -1.0, 128.0, A.mult, A.add)
-    for i in range(2, 4):
-        quant("qv%d" % i, ["v1"], "qv", 128 * i, T.vb[:, 512 * i:512 * i + 512])
+    op("v", ["jm", "pif"], ["h1z"], V.tensor_scalar, T.h1[:, 2:512:4], T.jm[:], T.pif[:, 0:1], None, A.is_equal)
+    op("v", ["jm", "pif"], wp, V.tensor_scalar, T.wp[:, 2:512:4], T.jm[:], T.pif[:, 0:1], 256.0, A.not_equal, A.mult)
     op("v", ["gs", "pm0"], ["ca"], V.tensor_scalar, T.ca[:], T.gs[:], T.pm0[:, 0:1], 1.0 / 128, A.add, A.mult)
+    op("v", ["gs", "pm0"], ["cx"], V.tensor_scalar, T.cx[:], T.gs[:], T.pm0[:, 0:1], C - 128.0, A.add, A.add)
     op("g", ["ca"], ["cb"], g.affine_select, T.cb[:], T.ca[:], [[0, 8], [1, 16]], A.is_equal, -1.0, 0, 0)
-    pick("up", ["tu", "z8"], "up", 128, 0, "tu", 0, 1, T.z8[:, 0:8])
+    op("g", ["cx"], ["cr"], g.affine_select, T.cr[:], T.cx[:], [[0, 8], [1, 16]], A.is_equal, 0.0, 0, 0)
+    op("v", ["jm", "pm0"], ["thr"], V.tensor_scalar, T.thr[:], T.jm[:], T.pm0[:, 0:1], float(C), A.is_equal, A.mult)
+    quant("qk", wp, "qk", 0, T.wp[:])
+    for i in range(4):
+        quant("qv%d" % i, ["v%d" % (i // 2)], "qv", 128 * i, T.vb[:, 512 * i:512 * i + 512])
+    up = ("up", 128, 0, "tu", 0, 1, T.z8[:, 0:8])
+    pick_codes("up", ["tu", "z8"], *up)
 
     def mm(reads, bank, w, a, x, b):
         op("t", reads, [bank], E.matmul_mx, T[bank][:, 0:128], T[w][:, a:a + 128], T[w + "s"][:, a:a + 128],
@@ -196,10 +195,10 @@ def rank_program(g, core, T, topo):
         op("v", ["later", "p0"], ["sm"], V.tensor_scalar, T.sm[:], T.later[:], T.p0[:, 0:1], None, A.add)
         op("v", ["p0", "p1"], ["h1"], V.tensor_scalar, T.h1[:, 0:512:4], T.p1[:, 0:128], T.p0[:, 0:1], None, A.is_lt)
         op("v", ["sm", "p1"], ["h1e"], V.tensor_tensor, T.h1[:, 1:512:4], T.p1[:, 0:128], T.sm[:], A.is_equal)
-        quant(qh, ["h1", "h1e"], qh, 0, T.h1[:])
+        quant(qh, ["h1", "h1e", "h1z", "h1y"], qh, 0, T.h1[:])
 
-    def ranks(qh, bank):
-        mm(["qo", qh], bank, "qo", 0, qh, 0)
+    def ranks(qh, bank, w="qo"):
+        mm([w, qh], bank, w, 0, qh, 0)
 
     def row(i, bank, t, tk, at):
         mm(["qv%d" % i] + tk, bank, "qv", 128 * i, t, at)
@@ -214,61 +213,64 @@ def rank_program(g, core, T, topo):
         op("v", [bank, r + str(i)], [n + str(i)], V.tensor_tensor, T[n][:, i:512:4], T[bank][:, 0:128],
            T[r][:, 128 * i:128 * i + 128], A.add)
 
-    def places(name):
-        op("v", ["p2", "pif"], ["nl"], V.tensor_scalar, T.nl[0:C, :], T.p2[0:C, 0:128], T.pif[0:C, 0:1], None, A.not_equal)
-        op("v", ["nl", "on"], ["sl"], V.tensor_tensor_scan, T.sl[0:C, :], T.nl[0:C, :], T.on[0:C, 0:128], 0.0, A.mult, A.add)
-        op("v", ["sl"], [name], V.tensor_scalar, T[name][0:C, 0:1], T.sl[0:C, 127:128], -1.0, 128.0, A.mult, A.add)
+    def place(k, bank, name):
+        if k == 0:
+            op("v", [bank, "pif"], ["nl"], V.tensor_scalar, T.nl[0:C, :], T[bank][0:C, 0:128], T.pif[0:C, 0:1], None, A.not_equal)
+        elif k == 1:
+            op("v", ["nl"] + on, ["sl"], V.tensor_tensor_scan, T.sl[0:C, :], T.nl[0:C, :], T.on[0:C, 0:128], 0.0, A.mult, A.add)
+        else:
+            op("v", ["sl"], [name], V.tensor_scalar, T[name][0:C, 0:1], T.sl[0:C, 127:128], -1.0, 128.0, A.mult, A.add)
 
-    def first_half(t, tk, at, r, n, qh):
+    def first_half(t, tk, at, r, n, qh, bank):
         row(0, "p3", t, tk, at)
         row(1, "p4", t, tk, at)
         old(0, "p5", t, tk, at)
         old(1, "p6", t, tk, at)
         row(2, "p7", t, tk, at)
-        compare(qh)
-        ranks(qh, "p2")
         for i, b in enumerate(["p3", "p4", "p7"]):
             relu(i, b, r)
-        row(3, "p0", t, tk, at)
         old(2, "p3", t, tk, at)
+        compare(qh)
+        ranks(qh, bank)
+        row(3, "p0", t, tk, at)
         old(3, "p4", t, tk, at)
         relu(3, "p0", r)
         add(0, "p5", r, n)
         add(1, "p6", r, n)
 
     scores("ur", "ta", ["ta"])
-    first_half("ta", ["ta"], 0, "ra", "n1", "qh1")
+    first_half("ta", ["ta"], 0, "ra", "n1", "qh1", "p2")
+    pick_scales("up", ["tus", "z8"], *up)
     op("v", ["p2", "pm0"], ["nb0"], V.tensor_scalar, T.nb[:, 0:128], T.p2[:, 0:128], T.pm0[:, 0:1], None, A.not_equal)
     op("v", ["p2", "pm1"], ["nb1"], V.tensor_scalar, T.nb[:, 128:256], T.p2[:, 0:128], T.pm1[:, 0:1], None, A.not_equal)
     add(2, "p3", "ra", "n1")
-    op("v", ["nb0", "nb1", "on"], ["sc"], V.tensor_tensor_scan, T.sc[:], T.nb[:], T.on[:], 0.0, A.mult, A.add)
+    op("v", ["nb0", "nb1"] + on, ["sc"], V.tensor_tensor_scan, T.sc[:], T.nb[:], T.on[:], 0.0, A.mult, A.add)
     add(3, "p4", "ra", "n1")
     op("v", ["sc"], ["lst"], V.tensor_scalar, T.lst[:], T.sc[:, 127:256:128], -1.0, 128.0, A.mult, A.add)
     quant("qn", ["n1%d" % i for i in range(4)], "qn", 0, T.n1[:])
     pick("pk", ["qn", "lst"], "pk", 32, 0, "qn", 0, 128, T.lst[:, 0:2])
-    send(["pk"], nxt, code("tb", 128, 160), code("pk", 0, 32), "arrn")
-    send(["pks"], nxt, T.tbs[:, 128:160], T.pks[:, 0:32], "arrn")
+    send(["pk"], nxt, code("tb", 0, C), code("pk", 0, 32), "arrn")
+    send(["pks"], nxt, T.tbs[:, 0:C], T.pks[:, 0:32], "arrn")
 
-    scores("up", "tb", ["tb"])
+    scores("up", "tb", ["tb"], C)
     compare("qh2")
-    ranks("qh2", "p2")
-    op("v", ["jm", "pm0"], ["thr"], V.tensor_scalar, T.thr[:], T.jm[:], T.pm0[:, 0:1], float(C), A.is_equal, A.mult)
-    op("v", ["p2", "km"], ["mk"], V.tensor_tensor, T.mk[:], T.p2[:, 0:128], T.km[:], A.max)
-    op("v", ["cr", "mk"], ["r8"], V.tensor_tensor_scan, T.r8[:], T.cr[:], T.mk[:], 256.0, A.max, A.min)
-    op("v", ["r8"], ["c8"], V.tensor_scalar, T.c8[:], T.r8[:, 15:128:16], float(C), None, A.is_lt)
-    op("v", ["r8", "jr"], ["d8"], V.tensor_tensor, T.d8[:], T.r8[:, 15:128:16], T.jr[:], A.add)
-    op("v", ["c8", "d8"], ["e8"], V.tensor_tensor, T.e8[:], T.c8[:], T.d8[:], A.mult)
-    op("v", ["e8", "j8"], ["f8"], V.tensor_tensor, T.f8[:], T.e8[:], T.j8[:], A.add)
-    op("v", ["f8"], ["off1"], V.tensor_copy, T.off1[:], T.f8[:])
+    ranks("qh2", "p2", "qk")
+    ranks("qh2", "p4")
     quant("qw", ["w"], "qw", 0, T.wb[:])
-    places("li0")
+    op("v", ["p2"], ["mk"], V.tensor_scalar, T.mk[:], T.p2[:, 0:128], 0.5 - C, 1024.0, A.add, A.mult)
+    place(0, "p4", "li0")
+    op("v", ["p2", "mk"], ["ml"], V.tensor_tensor, T.ml[:], T.p2[:, 0:128], T.mk[:], A.max)
+    place(1, "p4", "li0")
+    op("v", ["cr", "ml"], ["r8"], V.tensor_tensor_scan, T.r8[:], T.cr[:], T.ml[:], 0.0, A.max, A.min)
+    place(2, "p4", "li0")
+    op("v", ["r8"], ["off1"], V.tensor_copy, T.off1[:], T.r8[:, 15:128:16])
     dma("y", "dl0", ["li0"], [], T.li[0:1, 0:C], T.li0[0:C, 0:1])
 
     pick("t1", ["tb", "tn", "off1"], "win", 128, 128, "tb", 0, 160, T.off1[:, 0:8])
     tk = ["t1", "t1s"]
     scores("ur", "win", tk, 128)
-    first_half("win", tk, 128, "rb", "n2", "qh3")
-    op("v", ["p2", "thr"], ["fl"], V.tensor_tensor, T.fl[:], T.p2[:, 0:128], T.thr[:], A.is_lt)
+    first_half("win", tk, 128, "rb", "n2", "qh3", "p1")
+    op("v", ["p1", "thr"], ["fl"], V.tensor_tensor, T.fl[:], T.p1[:, 0:128], T.thr[:], A.is_lt)
     add(2, "p3", "rb", "n2")
     op("v", ["cb", "fl"], ["st"], V.tensor_tensor_scan, T.st[:], T.cb[:], T.fl[:], 0.0, A.max, A.subtract)
     add(3, "p4", "rb", "n2")
@@ -278,7 +280,8 @@ def rank_program(g, core, T, topo):
 
     mm(["qw", "t2", "t2s"], "p4", "qw", 0, "t2", 0)
     op("s", ["p4"], ["ys"], S.activation, T.ys[:], T.p4[:, 0:128], F.Copy)
-    places("li1")
+    for k in range(3):
+        place(k, "p1", "li1")
     dma("y", "do", ["t2"], [], T.oc[:, 0:512], code("t2", 0, 128))
     for k in range(4):
         dma("y", "ds%d" % k, ["t2s"], [], T.osc[4 * k:4 * k + 4, 0:128], T.t2s[32 * k:32 * k + 4, 0:128])

@@ -3,7 +3,8 @@ from concourse.mybir import dt, AluOpType, ActivationFunctionType
 N = 8
 C = 32
 FACTOR = 13421773 * 2.0 ** -28
-FAR = 1.0e29
+UNIT = 1.0 / 256
+TIE = 2.0 ** -100
 
 SCRATCH = {}
 
@@ -19,28 +20,32 @@ def _pair(width, *names):
         _declare("uint8", width, n + "s")
 
 
-_declare("bfloat16", 512, "xb", "ub", "wb", "wo", "wp", "h1", "n1", "n2")
+_declare("bfloat16", 512, "xb", "ub", "wb", "wo", "h1", "n1", "n2")
 _declare("bfloat16", 2048, "vb")
 _declare("bfloat16", 520, "eb")
-_declare("bfloat16", 128, "ob", "idn", "thr", "cr", "cx", "ca", "cb", "mk", "ml", "r8", "fl", "st", "nl", "sl")
-_declare("bfloat16", 256, "on", "nb", "sc")
-_declare("float32", 128, "zf", "later", "jm", "gs", "sm", "ys")
+_declare("bfloat16", 128, "ob", "zf", "idn", "tie", "dn", "jm", "far", "thr", "cr", "cb", "ml", "q1", "r8", "fl", "st",
+         "nl0", "nl1", "sl0", "sl1")
+_declare("bfloat16", 256, "nb", "sc")
+_declare("float32", 128, "ys")
 _declare("float32", 512, "ra", "rb")
-_declare("float32", 1, "pif", "pm0", "pm1", "li0", "li1")
+_declare("float32", 1, "pif", "pm0", "pa0", "pa1", "pb", "pc", "pnp", "li0", "li1")
+_declare("float32", 8, "gs")
 _declare("int32", 1, "pii", "pmi")
-_declare("uint16", 8, "z8", "off1", "off2")
+_declare("uint16", 16, "rep")
+_declare("uint16", 8, "off1", "off2")
 _declare("uint16", 2, "lst")
 _pair(512, "qv", "qe")
-_pair(256, "win")
+_pair(256, "win", "qx", "ur", "up")
 _pair(160, "tb")
-_pair(128, "qx", "qu", "qw", "qo", "qk", "ur", "up", "ta", "qh1", "qh2", "qh3", "qn", "t2")
-_pair(32, "tu", "pk")
+_pair(130, "ta")
+_pair(128, "qw", "qo", "qh1", "qh2", "qh3", "qn", "t2")
+_pair(32, "pk")
 for _i in range(8):
     SCRATCH["p%d" % _i] = ("psum", [128, 512], "float32")
 
 LOADS = ["dx", "du", "dv0", "dv1", "dw"]
 STORES = ["do", "ds0", "ds1", "ds2", "ds3", "dy", "dl0", "dl1"]
-SEMAPHORES = ["cv", "cs", "ct", "cg", "sent", "arru", "arrs", "arra", "arrb", "arrn"] + LOADS + STORES
+SEMAPHORES = ["cv", "cs", "ct", "cg", "sent", "arru", "arra", "arrb", "arrn"] + LOADS + STORES
 
 
 def rank_program(g, core, T, topo):
@@ -73,12 +78,15 @@ def rank_program(g, core, T, topo):
             wrote[k] = ev
             read[k] = []
 
-    def op(q, reads, writes, call, *args, **kw):
-        ready(q, reads, writes)
+    def issue(q, reads, writes, call, *args, **kw):
         count[q] += 1
         order[0] += 1
         call(*args, **kw).then_inc(T.sem[counter[q]], 1)
         done(q, (order[0], counter[q], count[q], dict(known[q])), reads, writes)
+
+    def op(q, reads, writes, call, *args, **kw):
+        ready(q, reads, writes)
+        issue(q, reads, writes, call, *args, **kw)
 
     def dma(q, sem, reads, writes, out, in_):
         ready(q, reads, writes)
@@ -103,8 +111,7 @@ def rank_program(g, core, T, topo):
         g.remote_dma(out_ap=out, in_ap=in_, remote_sem=T.sem[sem], local_sem=T.sem.sent, pid=pid, routing_id=rid,
                      dma_engine_mask=sum(1 << e for e in es))
 
-    for key, sem, src, calls in (("tu", "arru", prv, 1), ("tus", "arrs", prv, 1), ("ta", "arra", prv, 2),
-                                 ("tb", "arrb", prv2, 2), ("tn", "arrn", prv, 2)):
+    for key, sem, src, calls in (("tu", "arru", prv, 1), ("ta", "arra", prv, 2), ("tb", "arrb", prv2, 2), ("tn", "arrn", prv, 2)):
         wrote[key] = (0, sem, calls * len(lanes(src, core)), {})
 
     def code(name, a, b):
@@ -112,6 +119,9 @@ def rank_program(g, core, T, topo):
 
     def quant(key, reads, name, a, in_):
         op("v", reads, [key], V.quantize_mx, T[name][:, a:a + 128], T[name + "s"][:, a:a + 128], in_)
+
+    def act(reads, key, out, in_, func, **kw):
+        op("s", reads, [key], S.activation, out, in_, func, **kw)
 
     def pick_codes(key, reads, dst, n, at, src, a, b, off):
         op("v", reads, [key], V.tensor_copy, T[dst][:, at:at + n].bitcast(dt.uint32), T[src][:, a:b].bitcast(dt.uint32).indirect(off))
@@ -123,82 +133,87 @@ def rank_program(g, core, T, topo):
         pick_codes(*args)
         pick_scales(*args)
 
-    dma("s", "du", [], ["u"], T.ub[:, 0:8], T.u[:, 0:8])
+    dma("s", "du", [], ["u"], T.ub[:, 0:4], T.u[:, 0:4])
     dma("y", "dx", [], ["x"], T.xb[:], T.x[:, 0:512])
     dma("y", "dv0", [], ["v0"], T.vb[:, 0:1024], T.v[:, 0:1024])
-    dma("y", "dv1", [], ["v1"], T.vb[:, 1024:2048], T.v[:, 1024:2048])
-    dma("y", "dw", ["tu"], ["w"], T.wb[:], T.w[:, 0:512])
+    dma("y", "dv1", ["tu"], ["v1"], T.vb[:, 1024:2048], T.v[:, 1024:2048])
+    dma("y", "dw", ["ta"], ["w"], T.wb[:], T.w[:, 0:512])
 
     small = dict(allow_small_or_imprecise_dtypes=True)
     op("v", [], ["ob"], V.memset, T.ob[:], 1.0)
-    op("v", [], ["zf"], V.memset, T.zf[:], 0.0)
     op("g", ["ob"], ["idn"], g.affine_select, T.idn[:], T.ob[:], [[-1, 128]], A.is_equal, 0.0, 0, 1)
     op("g", [], ["pii"], g.iota, T.pii[:], [[0, 1]], 0, 1)
-    op("g", [], ["jm"], g.iota, T.jm[:], [[0, 8], [1, 16]], 0, 0, **small)
     op("g", [], ["pif"], g.iota, T.pif[:], [[0, 1]], 0, 1, **small)
-    op("g", [], ["gs"], g.iota, T.gs[:], [[16, 8], [0, 16]], 128, 0, **small)
-    op("g", ["zf"], ["later"], g.affine_select, T.later[:], T.zf[:], [[1, 128]], A.is_gt, FAR, 0, -1)
+    op("g", [], ["gs"], g.iota, T.gs[:], [[16, 8]], 128, 0, **small)
 
-    def ones(name, width, first=0):
-        keys = [name + str(i) for i in range(width // 128)]
-        for i, k in enumerate(keys):
-            a, b = max(first, 128 * i), 128 * i + 128
-            op("s", ["ob"], [k], S.activation, T[name][:, a:b], T.ob[:, 0:b - a], F.Copy)
-        return keys
+    for i in range(4):
+        a, b = max(8, 128 * i), 128 * i + 128
+        act(["ob"], "ub%d" % i, T.ub[:, a:b], T.ob[:, 0:b - a], F.Copy)
+    act(["u"], "nu", T.ub[:, 4:8], T.ub[:, 0:4], F.Copy, scale=-1.0)
+    ub = ["u", "nu"] + ["ub%d" % i for i in range(4)]
 
-    uz = ones("ub", 512, 8)
-    wo, wp, on = ones("wo", 512), ones("wp", 512), ones("on", 256)
     op("v", [], ["eb"], V.memset, T.eb[:], 0.0)
-    op("v", [], ["z8"], V.memset, T.z8[:], 0)
-    op("v", [], ["h1y"], V.memset, T.h1[:, 3:512:4], 0.0)
+    op("v", [], ["zf"], V.memset, T.zf[:], 0.0)
+    op("v", [], ["rep0"], V.memset, T.rep[:, 0:8], 0)
+    op("v", [], ["rep1"], V.memset, T.rep[:, 8:16], 1)
     op("v", ["idn"], ["eb"], V.tensor_copy, T.eb[:, 3:515:4], T.idn[:])
-    for b in range(4):
-        quant("qe%d" % b, ["eb"], "qe", 128 * b, T.eb[:, 3 - b:515 - b])
-    op("v", ["pii"], ["pmi"], V.tensor_scalar, T.pmi[:], T.pii[:], 15, None, A.bitwise_and)
-    op("v", [], wo, V.memset, T.wo[:, 2:512:4], 0.0)
-    op("v", ["pmi"], ["pm0"], V.tensor_copy, T.pm0[:], T.pmi[:])
-    quant("qo", wo, "qo", 0, T.wo[:])
-    op("v", ["pm0"], ["pm1"], V.tensor_scalar, T.pm1[:], T.pm0[:], 16.0, None, A.add)
+    op("v", [], ["h1"], V.memset, T.h1[:], 0.0)
 
-    quant("qu", ["u"] + uz, "qu", 0, T.ub[:])
+    quant("qu", ub, "qx", 128, T.ub[:])
     quant("qx", ["x"], "qx", 0, T.xb[:])
-    send(["qu"], nxt, code("tu", 0, 1), code("qu", 0, 1), "arru")
+    send(["qu"], nxt, code("ta", 128, 130), code("qx", 128, 130), "arru")
     send(["qx"], nxt, code("ta", 0, 128), code("qx", 0, 128), "arra")
-    send(["qx"], nxt, T.tas[:, 0:128], T.qxs[:, 0:128], "arra")
-    send(["qu"], nxt, T.tus[:, 0:2], T.qus[:, 0:2], "arrs")
+    send(["qx", "qu"], nxt, T.tas[:, 0:130], T.qxs[:, 0:130], "arra")
+    op("g", ["zf"], ["tie"], g.affine_select, T.tie[:], T.zf[:], [[-1, 128]], A.is_ge, TIE, 0, 1)
+    op("g", [], ["dn"], g.iota, T.dn[:], [[-1, 128]], 128, 0, **small)
+    op("g", [], ["jm"], g.iota, T.jm[:], [[0, 8], [1, 16]], 0, 0, **small)
+    ready("g", ["ta"], [])
     send(["qx"], nxt2, code("tb", C, C + 128), code("qx", 0, 128), "arrb")
     send(["qx"], nxt2, T.tbs[:, C:C + 128], T.qxs[:, 0:128], "arrb")
 
-    pick("ur", ["qu", "z8"], "ur", 128, 0, "qu", 0, 1, T.z8[:, 0:8])
-    op("v", ["jm", "pif"], ["h1z"], V.tensor_scalar, T.h1[:, 2:512:4], T.jm[:], T.pif[:, 0:1], None, A.is_equal)
-    op("v", ["jm", "pif"], wp, V.tensor_scalar, T.wp[:, 2:512:4], T.jm[:], T.pif[:, 0:1], 256.0, A.not_equal, A.mult)
-    op("v", ["gs", "pm0"], ["ca"], V.tensor_scalar, T.ca[:], T.gs[:], T.pm0[:, 0:1], 1.0 / 128, A.add, A.mult)
-    op("v", ["gs", "pm0"], ["cx"], V.tensor_scalar, T.cx[:], T.gs[:], T.pm0[:, 0:1], C - 128.0, A.add, A.add)
-    op("g", ["ca"], ["cb"], g.affine_select, T.cb[:], T.ca[:], [[0, 8], [1, 16]], A.is_equal, -1.0, 0, 0)
-    op("g", ["cx"], ["cr"], g.affine_select, T.cr[:], T.cx[:], [[0, 8], [1, 16]], A.is_equal, 0.0, 0, 0)
-    op("v", ["jm", "pm0"], ["thr"], V.tensor_scalar, T.thr[:], T.jm[:], T.pm0[:, 0:1], float(C), A.is_equal, A.mult)
-    quant("qk", wp, "qk", 0, T.wp[:])
+    ur = ("ur", 256, 0, "qx", 128, 130, T.rep[:, 0:16])
+    up = ("up", 256, 0, "ta", 128, 130, T.rep[:, 0:16])
     for i in range(4):
-        quant("qv%d" % i, ["v%d" % (i // 2)], "qv", 128 * i, T.vb[:, 512 * i:512 * i + 512])
-    up = ("up", 128, 0, "tu", 0, 1, T.z8[:, 0:8])
-    pick_codes("up", ["tu", "z8"], *up)
+        act(["ob"], "wo%d" % i, T.wo[:, 128 * i:128 * i + 128], T.ob[:], F.Copy, scale=UNIT)
+    pick("ur", ["qu", "rep0", "rep1"], *ur[1:]) if False else pick(ur[0], ["qu", "rep0", "rep1"], *ur)
+    op("v", ["pii"], ["pmi"], V.tensor_scalar, T.pmi[:], T.pii[:], 15, None, A.bitwise_and)
+    for b in range(4):
+        quant("qe%d" % b, ["eb"], "qe", 128 * b, T.eb[:, 3 - b:515 - b])
+    op("v", ["pmi"], ["pm0"], V.tensor_copy, T.pm0[:], T.pmi[:])
+    quant("qv0", ["v0"], "qv", 0, T.vb[:, 0:512])
+    quant("qv1", ["v0"], "qv", 128, T.vb[:, 512:1024])
+    quant("qo", ["wo%d" % i for i in range(4)], "qo", 0, T.wo[:])
+    pick_codes("up", ["tu", "rep0", "rep1"], *up)
+    act(["pm0"], "pa0", T.pa0[:], T.pm0[:], F.Copy, scale=UNIT)
+    act(["pm0"], "pa1", T.pa1[:], T.pm0[:], F.Copy, scale=UNIT, bias=16 * UNIT)
+    act(["pif"], "pnp", T.pnp[:], T.pif[:], F.Copy, scale=-256.0)
+    act(["pm0"], "pb", T.pb[:], T.pm0[:], F.Copy, scale=1.0 / 128)
+    act(["pm0"], "pc", T.pc[:], T.pm0[:], F.Copy, scale=UNIT, bias=(C - 128) * UNIT)
+    act(["jm", "pm0"], "far", T.far[:], T.jm[:], F.Abs, scale=-1.0, bias=T.pm0[:, 0:1])
+    act(["far"], "thr", T.thr[:], T.far[:], F.Relu, scale=-C * UNIT, bias=C * UNIT)
+    act(["zf"], "cr", T.cr[:], T.zf[:], F.Copy)
+    act(["gs", "pc"], "cr", T.cr[:, 0:128:16], T.gs[:], F.Identity, scale=UNIT, bias=T.pc[:, 0:1])
+    act(["zf"], "cb", T.cb[:], T.zf[:], F.Copy, bias=-1.0)
+    act(["gs", "pb"], "cb", T.cb[:, 0:128:16], T.gs[:], F.Identity, scale=1.0 / 128, bias=T.pb[:, 0:1])
 
     def mm(reads, bank, w, a, x, b):
         op("t", reads, [bank], E.matmul_mx, T[bank][:, 0:128], T[w][:, a:a + 128], T[w + "s"][:, a:a + 128],
            T[x][:, b:b + 128], T[x + "s"][:, b:b + 128], True, True)
 
     def scores(u, t, tk, at=0):
-        mm([u, u + "s"] + tk, "p0", t, at, u, 0)
-        mm([u, u + "s"] + tk, "p1", u, 0, t, at)
+        reads = [u, u + "s"] + tk
+        ready("t", reads, ["p0"])
+        issue("t", reads, ["p0"], E.matmul_mx, T.p0[:, 0:128], T[t][:, at:at + 128], T[t + "s"][:, at:at + 128],
+              T[u][:, 128:256], T[u + "s"][:, 128:256], True, False)
+        issue("t", reads, ["p0"], E.matmul_mx, T.p0[:, 0:128], T[u][:, 0:128], T[u + "s"][:, 0:128],
+              T[t][:, at:at + 128], T[t + "s"][:, at:at + 128], False, True)
 
     def compare(qh):
-        op("v", ["later", "p0"], ["sm"], V.tensor_scalar, T.sm[:], T.later[:], T.p0[:, 0:1], None, A.add)
-        op("v", ["p0", "p1"], ["h1"], V.tensor_scalar, T.h1[:, 0:512:4], T.p1[:, 0:128], T.p0[:, 0:1], None, A.is_lt)
-        op("v", ["sm", "p1"], ["h1e"], V.tensor_tensor, T.h1[:, 1:512:4], T.p1[:, 0:128], T.sm[:], A.is_equal)
-        quant(qh, ["h1", "h1e", "h1z", "h1y"], qh, 0, T.h1[:])
+        op("v", ["tie", "p0"], ["h1"], V.tensor_tensor, T.h1[:, 0:512:4], T.p0[:, 0:128], T.tie[:], A.is_lt)
+        quant(qh, ["h1"], qh, 0, T.h1[:])
 
-    def ranks(qh, bank, w="qo"):
-        mm([w, qh], bank, w, 0, qh, 0)
+    def ranks(qh, bank):
+        mm(["qo", qh], bank, "qo", 0, qh, 0)
 
     def row(i, bank, t, tk, at):
         mm(["qv%d" % i] + tk, bank, "qv", 128 * i, t, at)
@@ -207,46 +222,54 @@ def rank_program(g, core, T, topo):
         mm(["qe%d" % i] + tk, bank, "qe", 128 * i, t, at)
 
     def relu(i, bank, r):
-        op("s", [bank], [r + str(i)], S.activation, T[r][:, 128 * i:128 * i + 128], T[bank][:, 0:128], F.Relu, scale=FACTOR)
+        act([bank], r + str(i), T[r][:, 128 * i:128 * i + 128], T[bank][:, 0:128], F.Relu, scale=FACTOR)
 
     def add(i, bank, r, n):
         op("v", [bank, r + str(i)], [n + str(i)], V.tensor_tensor, T[n][:, i:512:4], T[bank][:, 0:128],
            T[r][:, 128 * i:128 * i + 128], A.add)
 
-    def place(k, bank, name):
-        if k == 0:
-            op("v", [bank, "pif"], ["nl"], V.tensor_scalar, T.nl[0:C, :], T[bank][0:C, 0:128], T.pif[0:C, 0:1], None, A.not_equal)
-        elif k == 1:
-            op("v", ["nl"] + on, ["sl"], V.tensor_tensor_scan, T.sl[0:C, :], T.nl[0:C, :], T.on[0:C, 0:128], 0.0, A.mult, A.add)
-        else:
-            op("v", ["sl"], [name], V.tensor_scalar, T[name][0:C, 0:1], T.sl[0:C, 127:128], -1.0, 128.0, A.mult, A.add)
+    def scan(reads, key, out, marks, rows=128):
+        op("v", reads + ["dn"], [key], V.tensor_tensor_scan, out, marks, T.dn[0:rows, :], 200.0, A.min, A.max)
 
-    def first_half(t, tk, at, r, n, qh, bank):
-        row(0, "p3", t, tk, at)
-        row(1, "p4", t, tk, at)
-        old(0, "p5", t, tk, at)
-        old(1, "p6", t, tk, at)
-        row(2, "p7", t, tk, at)
-        for i, b in enumerate(["p3", "p4", "p7"]):
-            relu(i, b, r)
-        old(2, "p3", t, tk, at)
-        compare(qh)
-        ranks(qh, bank)
-        row(3, "p0", t, tk, at)
-        old(3, "p4", t, tk, at)
-        relu(3, "p0", r)
-        add(0, "p5", r, n)
-        add(1, "p6", r, n)
+    def li_mark(k, bank):
+        act([bank, "pnp"], "nl%d" % k, T["nl%d" % k][0:C, :], T[bank][0:C, 0:128], F.Abs, scale=65536.0, bias=T.pnp[0:C, 0:1])
 
-    scores("ur", "ta", ["ta"])
-    first_half("ta", ["ta"], 0, "ra", "n1", "qh1", "p2")
-    pick_scales("up", ["tus", "z8"], *up)
-    op("v", ["p2", "pm0"], ["nb0"], V.tensor_scalar, T.nb[:, 0:128], T.p2[:, 0:128], T.pm0[:, 0:1], None, A.not_equal)
-    op("v", ["p2", "pm1"], ["nb1"], V.tensor_scalar, T.nb[:, 128:256], T.p2[:, 0:128], T.pm1[:, 0:1], None, A.not_equal)
-    add(2, "p3", "ra", "n1")
-    op("v", ["nb0", "nb1"] + on, ["sc"], V.tensor_tensor_scan, T.sc[:], T.nb[:], T.on[:], 0.0, A.mult, A.add)
-    add(3, "p4", "ra", "n1")
-    op("v", ["sc"], ["lst"], V.tensor_scalar, T.lst[:], T.sc[:, 127:256:128], -1.0, 128.0, A.mult, A.add)
+    def li_scan(k):
+        scan(["nl%d" % k], "sl%d" % k, T["sl%d" % k][0:C, :], T["nl%d" % k][0:C, :], C)
+
+    def li_store(k):
+        act(["sl%d" % k], "li%d" % k, T["li%d" % k][0:C, 0:1], T["sl%d" % k][0:C, 127:128], F.Copy, scale=-1.0, bias=128.0)
+        dma("y", "dl%d" % k, ["li%d" % k], [], T.li[k:k + 1, 0:C], T["li%d" % k][0:C, 0:1])
+
+    ta = ("ta", ["ta"], 0)
+    scores("ur", *ta)
+    row(0, "p3", *ta)
+    compare("qh1")
+    quant("qv2", ["v1"], "qv", 256, T.vb[:, 1024:1536])
+    quant("qv3", ["v1"], "qv", 384, T.vb[:, 1536:2048])
+    old(0, "p4", *ta)
+    row(1, "p5", *ta)
+    pick_scales("up", ["ta", "rep0", "rep1"], *up)
+    relu(0, "p3", "ra")
+    relu(1, "p5", "ra")
+    ranks("qh1", "p1")
+    old(1, "p6", *ta)
+    row(2, "p7", *ta)
+    row(3, "p3", *ta)
+    old(2, "p0", *ta)
+    old(3, "p5", *ta)
+    relu(2, "p7", "ra")
+    relu(3, "p3", "ra")
+    add(0, "p4", "ra", "n1")
+    for k in range(2):
+        op("v", ["p1", "pa%d" % k], ["nb%d" % k], V.tensor_scalar, T.nb[:, 128 * k:128 * k + 128], T.p1[:, 0:128],
+           T["pa%d" % k][:, 0:1], 512.0, A.not_equal, A.mult)
+    add(1, "p6", "ra", "n1")
+    scan(["nb0"], "sc0", T.sc[:, 0:128], T.nb[:, 0:128])
+    add(2, "p0", "ra", "n1")
+    scan(["nb1"], "sc1", T.sc[:, 128:256], T.nb[:, 128:256])
+    add(3, "p5", "ra", "n1")
+    op("v", ["sc0", "sc1"], ["lst"], V.tensor_scalar, T.lst[:], T.sc[:, 127:256:128], -1.0, 128.0, A.mult, A.add)
     quant("qn", ["n1%d" % i for i in range(4)], "qn", 0, T.n1[:])
     pick("pk", ["qn", "lst"], "pk", 32, 0, "qn", 0, 128, T.lst[:, 0:2])
     send(["pk"], nxt, code("tb", 0, C), code("pk", 0, 32), "arrn")
@@ -254,39 +277,54 @@ def rank_program(g, core, T, topo):
 
     scores("up", "tb", ["tb"], C)
     compare("qh2")
-    ranks("qh2", "p2", "qk")
-    ranks("qh2", "p4")
-    quant("qw", ["w"], "qw", 0, T.wb[:])
-    op("v", ["p2"], ["mk"], V.tensor_scalar, T.mk[:], T.p2[:, 0:128], 0.5 - C, 1024.0, A.add, A.mult)
-    place(0, "p4", "li0")
-    op("v", ["p2", "mk"], ["ml"], V.tensor_tensor, T.ml[:], T.p2[:, 0:128], T.mk[:], A.max)
-    place(1, "p4", "li0")
+    ranks("qh2", "p1")
+    ranks("qh2", "p2")
+    op("v", ["p1", "thr"], ["q1"], V.tensor_tensor, T.q1[:], T.p1[:, 0:128], T.thr[:], A.is_ge)
+    li_mark(0, "p2")
+    op("v", ["p1", "q1"], ["ml"], V.tensor_tensor, T.ml[:], T.p1[:, 0:128], T.q1[:], A.max)
     op("v", ["cr", "ml"], ["r8"], V.tensor_tensor_scan, T.r8[:], T.cr[:], T.ml[:], 0.0, A.max, A.min)
-    place(2, "p4", "li0")
-    op("v", ["r8"], ["off1"], V.tensor_copy, T.off1[:], T.r8[:, 15:128:16])
-    dma("y", "dl0", ["li0"], [], T.li[0:1, 0:C], T.li0[0:C, 0:1])
+    op("v", ["r8"], ["off1"], V.tensor_scalar, T.off1[:], T.r8[:, 15:128:16], 256.0, None, A.mult)
 
     pick("t1", ["tb", "tn", "off1"], "win", 128, 128, "tb", 0, 160, T.off1[:, 0:8])
-    tk = ["t1", "t1s"]
-    scores("ur", "win", tk, 128)
-    first_half("win", tk, 128, "rb", "n2", "qh3", "p1")
+    t1 = ("win", ["t1", "t1s"], 128)
+    scores("ur", *t1)
+    row(0, "p3", *t1)
+    old(0, "p4", *t1)
+    row(1, "p5", *t1)
+    li_scan(0)
+    quant("qw", ["w"], "qw", 0, T.wb[:])
+    compare("qh3")
+    li_store(0)
+    relu(0, "p3", "rb")
+    relu(1, "p5", "rb")
+    ranks("qh3", "p1")
+    old(1, "p6", *t1)
+    row(2, "p7", *t1)
+    row(3, "p3", *t1)
+    old(2, "p0", *t1)
+    old(3, "p5", *t1)
+    ranks("qh3", "p2")
+    relu(2, "p7", "rb")
+    relu(3, "p3", "rb")
+    li_mark(1, "p2")
+    add(0, "p4", "rb", "n2")
     op("v", ["p1", "thr"], ["fl"], V.tensor_tensor, T.fl[:], T.p1[:, 0:128], T.thr[:], A.is_lt)
-    add(2, "p3", "rb", "n2")
+    add(1, "p6", "rb", "n2")
     op("v", ["cb", "fl"], ["st"], V.tensor_tensor_scan, T.st[:], T.cb[:], T.fl[:], 0.0, A.max, A.subtract)
-    add(3, "p4", "rb", "n2")
+    add(2, "p0", "rb", "n2")
+    add(3, "p5", "rb", "n2")
     op("v", ["st"], ["off2"], V.tensor_scalar, T.off2[:], T.st[:, 15:128:16], 128.0, None, A.mult)
     quant("n2q", ["n2%d" % i for i in range(4)], "win", 0, T.n2[:])
-    pick("t2", tk + ["n2q", "off2"], "t2", 128, 0, "win", 0, 256, T.off2[:, 0:8])
+    pick("t2", ["t1", "t1s", "n2q", "off2"], "t2", 128, 0, "win", 0, 256, T.off2[:, 0:8])
+    li_scan(1)
 
     mm(["qw", "t2", "t2s"], "p4", "qw", 0, "t2", 0)
-    op("s", ["p4"], ["ys"], S.activation, T.ys[:], T.p4[:, 0:128], F.Copy)
-    for k in range(3):
-        place(k, "p1", "li1")
     dma("y", "do", ["t2"], [], T.oc[:, 0:512], code("t2", 0, 128))
+    op("v", ["p4"], ["ys"], V.tensor_copy, T.ys[:], T.p4[:, 0:128])
+    li_store(1)
+    dma("s", "dy", ["ys"], [], T.y[:, 0:128], T.ys[:])
     for k in range(4):
         dma("y", "ds%d" % k, ["t2s"], [], T.osc[4 * k:4 * k + 4, 0:128], T.t2s[32 * k:32 * k + 4, 0:128])
-    dma("s", "dy", ["ys"], [], T.y[:, 0:128], T.ys[:])
-    dma("y", "dl1", ["li1"], [], T.li[1:2, 0:C], T.li1[0:C, 0:1])
 
     for q in ("v", "s", "t", "g"):
         g.wait_ge(T.sem[counter[q]], count[q])

@@ -20,32 +20,27 @@ def _pair(width, *names):
         _declare("uint8", width, n + "s")
 
 
-_declare("bfloat16", 512, "xb", "ub", "wb", "wo", "h1", "n1", "n2")
+_declare("bfloat16", 512, "xb", "ub", "wb", "wo", "h1", "h2", "n1", "n2")
 _declare("bfloat16", 2048, "vb")
 _declare("bfloat16", 520, "eb")
-_declare("bfloat16", 128, "ob", "zf", "idn", "tie", "dn", "jm", "far", "thr", "cr", "cb", "ml", "q1", "r8", "fl", "st",
-         "nl0", "nl1", "sl0", "sl1")
-_declare("bfloat16", 256, "nb", "sc")
+_declare("bfloat16", 128, "ob", "zf", "idn", "tie", "dn", "jm", "far", "thr", "cb", "f1", "f2", "s1", "s2", "nl1", "nl2", "sl1", "sl2")
 _declare("float32", 128, "ys")
-_declare("float32", 512, "ra", "rb")
-_declare("float32", 1, "pif", "pm0", "pa0", "pa1", "pb", "pc", "pnp", "li0", "li1")
+_declare("float32", 512, "r1", "r2")
+_declare("float32", 1, "pif", "pm0", "pb", "pnp", "li1", "li2", "lr")
 _declare("float32", 8, "gs")
 _declare("int32", 1, "pii", "pmi")
 _declare("uint16", 16, "rep")
 _declare("uint16", 8, "off1", "off2")
-_declare("uint16", 2, "lst")
 _pair(512, "qv", "qe")
-_pair(256, "win", "qx", "ur", "up")
-_pair(160, "tb")
-_pair(130, "ta")
-_pair(128, "qw", "qo", "qh1", "qh2", "qh3", "qn", "t2")
-_pair(32, "pk")
+_pair(256, "win1", "win2")
+_pair(256, "ur")
+_pair(128, "qx", "qu", "qw", "qo", "qh1", "qh2", "t1", "t2")
 for _i in range(8):
     SCRATCH["p%d" % _i] = ("psum", [128, 512], "float32")
 
 LOADS = ["dx", "du", "dv0", "dv1", "dw"]
-STORES = ["do", "ds0", "ds1", "ds2", "ds3", "dy", "dl0", "dl1"]
-SEMAPHORES = ["cv", "cs", "ct", "cg", "sent", "arru", "arra", "arrb", "arrn"] + LOADS + STORES
+STORES = ["do", "ds0", "ds1", "ds2", "ds3", "dy", "dl1", "dl2"]
+SEMAPHORES = ["cv", "cs", "ct", "cg", "sent", "arr1", "arr2", "arrl"] + LOADS + STORES
 
 
 def rank_program(g, core, T, topo):
@@ -95,24 +90,24 @@ def rank_program(g, core, T, topo):
         done(q, (order[0], sem, 16, dict(known[q])), reads, writes)
 
     V, S, E = g.vector, g.scalar, g.tensor
-    nxt, nxt2 = T.cores[(rank + 1) % N], T.cores[(rank + 2) % N]
-    prv, prv2 = T.cores[(rank - 1) % N], T.cores[(rank - 2) % N]
+    nxt, prv = T.cores[(rank + 1) % N], T.cores[(rank - 1) % N]
 
-    def lanes(src, dst):
-        return topo.engines(src, dst)[:8]
+    def lanes(src, dst, part):
+        es = topo.engines(src, dst)
+        return {"first": es[:8], "last": es[-8:], "all": es}[part]
 
     sent = [0]
 
-    def send(reads, dst, out, in_, sem):
+    def send(reads, out, in_, sem, part):
         ready("g", reads, [])
-        rid, pid = topo.addr(dst, core)
-        es = lanes(core, dst)
+        rid, pid = topo.addr(nxt, core)
+        es = lanes(core, nxt, part)
         sent[0] += len(es)
         g.remote_dma(out_ap=out, in_ap=in_, remote_sem=T.sem[sem], local_sem=T.sem.sent, pid=pid, routing_id=rid,
                      dma_engine_mask=sum(1 << e for e in es))
 
-    for key, sem, src, calls in (("tu", "arru", prv, 1), ("ta", "arra", prv, 2), ("tb", "arrb", prv2, 2), ("tn", "arrn", prv, 2)):
-        wrote[key] = (0, sem, calls * len(lanes(src, core)), {})
+    for key, sem, parts in (("in1", "arr1", ("first", "last")), ("in2", "arr2", ("all", "all")), ("lr", "arrl", ("first",))):
+        wrote[key] = (0, sem, sum(len(lanes(prv, core, p)) for p in parts), {})
 
     def code(name, a, b):
         return T[name][:, a:b].bitcast(dt.uint8)
@@ -123,76 +118,55 @@ def rank_program(g, core, T, topo):
     def act(reads, key, out, in_, func, **kw):
         op("s", reads, [key], S.activation, out, in_, func, **kw)
 
-    def pick_codes(key, reads, dst, n, at, src, a, b, off):
-        op("v", reads, [key], V.tensor_copy, T[dst][:, at:at + n].bitcast(dt.uint32), T[src][:, a:b].bitcast(dt.uint32).indirect(off))
+    def pick(key, reads, dst, n, src, a, b, off):
+        op("v", reads, [key], V.tensor_copy, T[dst][:, 0:n].bitcast(dt.uint32), T[src][:, a:b].bitcast(dt.uint32).indirect(off))
+        op("s", reads, [key + "s"], S.activation, T[dst + "s"][:, 0:n], T[src + "s"][:, a:b].indirect(off), F.Copy)
 
-    def pick_scales(key, reads, dst, n, at, src, a, b, off):
-        op("s", reads, [key + "s"], S.activation, T[dst + "s"][:, at:at + n], T[src + "s"][:, a:b].indirect(off), F.Copy)
-
-    def pick(*args):
-        pick_codes(*args)
-        pick_scales(*args)
-
-    dma("s", "du", [], ["u"], T.ub[:, 0:4], T.u[:, 0:4])
     dma("y", "dx", [], ["x"], T.xb[:], T.x[:, 0:512])
+    dma("y", "du", [], ["u"], T.ub[:, 0:4], T.u[:, 0:4])
     dma("y", "dv0", [], ["v0"], T.vb[:, 0:1024], T.v[:, 0:1024])
-    dma("y", "dv1", ["tu"], ["v1"], T.vb[:, 1024:2048], T.v[:, 1024:2048])
-    dma("y", "dw", ["ta"], ["w"], T.wb[:], T.w[:, 0:512])
+    dma("y", "dv1", [], ["v1"], T.vb[:, 1024:2048], T.v[:, 1024:2048])
+    dma("y", "dw", ["in1"], ["w"], T.wb[:], T.w[:, 0:512])
 
     small = dict(allow_small_or_imprecise_dtypes=True)
     op("v", [], ["ob"], V.memset, T.ob[:], 1.0)
+    op("v", [], ["zf"], V.memset, T.zf[:], 0.0)
     op("g", ["ob"], ["idn"], g.affine_select, T.idn[:], T.ob[:], [[-1, 128]], A.is_equal, 0.0, 0, 1)
     op("g", [], ["pii"], g.iota, T.pii[:], [[0, 1]], 0, 1)
     op("g", [], ["pif"], g.iota, T.pif[:], [[0, 1]], 0, 1, **small)
     op("g", [], ["gs"], g.iota, T.gs[:], [[16, 8]], 128, 0, **small)
+    op("v", [], ["eb"], V.memset, T.eb[:], 0.0)
+    op("v", [], ["h1"], V.memset, T.h1[:], 0.0)
+    op("v", [], ["rep0"], V.memset, T.rep[:, 0:8], 0)
+    op("v", [], ["rep1"], V.memset, T.rep[:, 8:16], 1)
+    op("v", ["idn"], ["eb"], V.tensor_copy, T.eb[:, 3:515:4], T.idn[:])
+
+    quant("qx", ["x"], "qx", 0, T.xb[:])
+    send(["qx"], code("win1", 128, 256), code("qx", 0, 128), "arr1", "first")
+    send(["qx"], T.win1s[:, 128:256], T.qxs[:], "arr1", "last")
+    op("g", ["zf"], ["tie"], g.affine_select, T.tie[:], T.zf[:], [[-1, 128]], A.is_ge, TIE, 0, 1)
+    op("g", [], ["jm"], g.iota, T.jm[:], [[0, 8], [1, 16]], 0, 0, **small)
+    op("g", [], ["dn"], g.iota, T.dn[:], [[-1, 128]], 128, 0, **small)
 
     for i in range(4):
         a, b = max(8, 128 * i), 128 * i + 128
         act(["ob"], "ub%d" % i, T.ub[:, a:b], T.ob[:, 0:b - a], F.Copy)
     act(["u"], "nu", T.ub[:, 4:8], T.ub[:, 0:4], F.Copy, scale=-1.0)
-    ub = ["u", "nu"] + ["ub%d" % i for i in range(4)]
-
-    op("v", [], ["eb"], V.memset, T.eb[:], 0.0)
-    op("v", [], ["zf"], V.memset, T.zf[:], 0.0)
-    op("v", [], ["rep0"], V.memset, T.rep[:, 0:8], 0)
-    op("v", [], ["rep1"], V.memset, T.rep[:, 8:16], 1)
-    op("v", ["idn"], ["eb"], V.tensor_copy, T.eb[:, 3:515:4], T.idn[:])
-    op("v", [], ["h1"], V.memset, T.h1[:], 0.0)
-
-    quant("qu", ub, "qx", 128, T.ub[:])
-    quant("qx", ["x"], "qx", 0, T.xb[:])
-    send(["qu"], nxt, code("ta", 128, 130), code("qx", 128, 130), "arru")
-    send(["qx"], nxt, code("ta", 0, 128), code("qx", 0, 128), "arra")
-    send(["qx", "qu"], nxt, T.tas[:, 0:130], T.qxs[:, 0:130], "arra")
-    op("g", ["zf"], ["tie"], g.affine_select, T.tie[:], T.zf[:], [[-1, 128]], A.is_ge, TIE, 0, 1)
-    op("g", [], ["dn"], g.iota, T.dn[:], [[-1, 128]], 128, 0, **small)
-    op("g", [], ["jm"], g.iota, T.jm[:], [[0, 8], [1, 16]], 0, 0, **small)
-    ready("g", ["ta"], [])
-    send(["qx"], nxt2, code("tb", C, C + 128), code("qx", 0, 128), "arrb")
-    send(["qx"], nxt2, T.tbs[:, C:C + 128], T.qxs[:, 0:128], "arrb")
-
-    ur = ("ur", 256, 0, "qx", 128, 130, T.rep[:, 0:16])
-    up = ("up", 256, 0, "ta", 128, 130, T.rep[:, 0:16])
     for i in range(4):
         act(["ob"], "wo%d" % i, T.wo[:, 128 * i:128 * i + 128], T.ob[:], F.Copy, scale=UNIT)
-    pick("ur", ["qu", "rep0", "rep1"], *ur[1:]) if False else pick(ur[0], ["qu", "rep0", "rep1"], *ur)
+    quant("qu", ["u", "nu"] + ["ub%d" % i for i in range(4)], "qu", 0, T.ub[:])
+    pick("ur", ["qu", "rep0", "rep1"], "ur", 256, "qu", 0, 2, T.rep[:, 0:16])
     op("v", ["pii"], ["pmi"], V.tensor_scalar, T.pmi[:], T.pii[:], 15, None, A.bitwise_and)
     for b in range(4):
         quant("qe%d" % b, ["eb"], "qe", 128 * b, T.eb[:, 3 - b:515 - b])
     op("v", ["pmi"], ["pm0"], V.tensor_copy, T.pm0[:], T.pmi[:])
-    quant("qv0", ["v0"], "qv", 0, T.vb[:, 0:512])
-    quant("qv1", ["v0"], "qv", 128, T.vb[:, 512:1024])
     quant("qo", ["wo%d" % i for i in range(4)], "qo", 0, T.wo[:])
-    pick_codes("up", ["tu", "rep0", "rep1"], *up)
-    act(["pm0"], "pa0", T.pa0[:], T.pm0[:], F.Copy, scale=UNIT)
-    act(["pm0"], "pa1", T.pa1[:], T.pm0[:], F.Copy, scale=UNIT, bias=16 * UNIT)
+    for i in range(4):
+        quant("qv%d" % i, ["v%d" % (i // 2)], "qv", 128 * i, T.vb[:, 512 * i:512 * i + 512])
     act(["pif"], "pnp", T.pnp[:], T.pif[:], F.Copy, scale=-256.0)
     act(["pm0"], "pb", T.pb[:], T.pm0[:], F.Copy, scale=1.0 / 128)
-    act(["pm0"], "pc", T.pc[:], T.pm0[:], F.Copy, scale=UNIT, bias=(C - 128) * UNIT)
     act(["jm", "pm0"], "far", T.far[:], T.jm[:], F.Abs, scale=-1.0, bias=T.pm0[:, 0:1])
     act(["far"], "thr", T.thr[:], T.far[:], F.Relu, scale=-C * UNIT, bias=C * UNIT)
-    act(["zf"], "cr", T.cr[:], T.zf[:], F.Copy)
-    act(["gs", "pc"], "cr", T.cr[:, 0:128:16], T.gs[:], F.Identity, scale=UNIT, bias=T.pc[:, 0:1])
     act(["zf"], "cb", T.cb[:], T.zf[:], F.Copy, bias=-1.0)
     act(["gs", "pb"], "cb", T.cb[:, 0:128:16], T.gs[:], F.Identity, scale=1.0 / 128, bias=T.pb[:, 0:1])
 
@@ -200,131 +174,74 @@ def rank_program(g, core, T, topo):
         op("t", reads, [bank], E.matmul_mx, T[bank][:, 0:128], T[w][:, a:a + 128], T[w + "s"][:, a:a + 128],
            T[x][:, b:b + 128], T[x + "s"][:, b:b + 128], True, True)
 
-    def scores(u, t, tk, at=0):
-        reads = [u, u + "s"] + tk
+    def stop(k):
+        win, key, n, r, qh, h = "win%d" % k, "in%d" % k, "n%d" % k, "r%d" % k, "qh%d" % k, "h%d" % k
+        flag, state, off, nl = "f%d" % k, "s%d" % k, "off%d" % k, "nl%d" % k
+
+        def row(i, bank):
+            mm(["qv%d" % i, key], bank, "qv", 128 * i, win, 128)
+            act([bank], r + str(i), T[r][:, 128 * i:128 * i + 128], T[bank][:, 0:128], F.Relu, scale=FACTOR)
+
+        def old(i, bank):
+            mm(["qe%d" % i, key], bank, "qe", 128 * i, win, 128)
+
+        def add(i, bank):
+            op("v", [bank, r + str(i)], [n + str(i)], V.tensor_tensor, T[n][:, i:512:4], T[bank][:, 0:128],
+               T[r][:, 128 * i:128 * i + 128], A.add)
+
+        reads = ["ur", "urs", key]
         ready("t", reads, ["p0"])
-        issue("t", reads, ["p0"], E.matmul_mx, T.p0[:, 0:128], T[t][:, at:at + 128], T[t + "s"][:, at:at + 128],
-              T[u][:, 128:256], T[u + "s"][:, 128:256], True, False)
-        issue("t", reads, ["p0"], E.matmul_mx, T.p0[:, 0:128], T[u][:, 0:128], T[u + "s"][:, 0:128],
-              T[t][:, at:at + 128], T[t + "s"][:, at:at + 128], False, True)
+        issue("t", reads, ["p0"], E.matmul_mx, T.p0[:, 0:128], T[win][:, 128:256], T[win + "s"][:, 128:256],
+              T.ur[:, 128:256], T.urs[:, 128:256], True, False)
+        issue("t", reads, ["p0"], E.matmul_mx, T.p0[:, 0:128], T.ur[:, 0:128], T.urs[:, 0:128],
+              T[win][:, 128:256], T[win + "s"][:, 128:256], False, True)
+        row(0, "p3")
+        old(0, "p4")
+        row(1, "p5")
+        op("v", ["tie", "p0"], [h], V.tensor_tensor, T[h][:, 0:512:4], T.p0[:, 0:128], T.tie[:], A.is_lt)
+        quant(qh, [h], qh, 0, T[h][:])
+        mm(["qo", qh], "p1", "qo", 0, qh, 0)
+        old(1, "p6")
+        row(2, "p7")
+        row(3, "p3")
+        old(2, "p0")
+        old(3, "p5")
+        mm(["qo", qh], "p2", "qo", 0, qh, 0)
+        add(0, "p4")
+        op("v", ["p1", "thr"], [flag], V.tensor_tensor, T[flag][:], T.p1[:, 0:128], T.thr[:], A.is_lt)
+        add(1, "p6")
+        op("v", ["cb", flag], [state], V.tensor_tensor_scan, T[state][:], T.cb[:], T[flag][:], 0.0, A.max, A.subtract)
+        add(2, "p0")
+        add(3, "p5")
+        op("v", [state], [off], V.tensor_scalar, T[off][:], T[state][:, 15:128:16], 128.0, None, A.mult)
+        quant("q" + n, [n + str(i) for i in range(4)], win, 0, T[n][:])
+        pick("t%d" % k, [key, "q" + n, off], "t%d" % k, 128, win, 0, 256, T[off][:])
+        act(["p2", "pnp"], nl, T[nl][:], T.p2[:, 0:128], F.Abs, scale=65536.0, bias=T.pnp[:, 0:1])
 
-    def compare(qh):
-        op("v", ["tie", "p0"], ["h1"], V.tensor_tensor, T.h1[:, 0:512:4], T.p0[:, 0:128], T.tie[:], A.is_lt)
-        quant(qh, ["h1"], qh, 0, T.h1[:])
+    def places(k):
+        nl, sl, li = "nl%d" % k, "sl%d" % k, "li%d" % k
+        op("v", [nl, "dn"], [sl], V.tensor_tensor_scan, T[sl][:], T[nl][:], T.dn[:], 200.0, A.min, A.max)
+        act([sl], li, T[li][:], T[sl][:, 127:128], F.Copy, scale=-1.0, bias=128.0)
 
-    def ranks(qh, bank):
-        mm(["qo", qh], bank, "qo", 0, qh, 0)
-
-    def row(i, bank, t, tk, at):
-        mm(["qv%d" % i] + tk, bank, "qv", 128 * i, t, at)
-
-    def old(i, bank, t, tk, at):
-        mm(["qe%d" % i] + tk, bank, "qe", 128 * i, t, at)
-
-    def relu(i, bank, r):
-        act([bank], r + str(i), T[r][:, 128 * i:128 * i + 128], T[bank][:, 0:128], F.Relu, scale=FACTOR)
-
-    def add(i, bank, r, n):
-        op("v", [bank, r + str(i)], [n + str(i)], V.tensor_tensor, T[n][:, i:512:4], T[bank][:, 0:128],
-           T[r][:, 128 * i:128 * i + 128], A.add)
-
-    def scan(reads, key, out, marks, rows=128):
-        op("v", reads + ["dn"], [key], V.tensor_tensor_scan, out, marks, T.dn[0:rows, :], 200.0, A.min, A.max)
-
-    def li_mark(k, bank):
-        act([bank, "pnp"], "nl%d" % k, T["nl%d" % k][0:C, :], T[bank][0:C, 0:128], F.Abs, scale=65536.0, bias=T.pnp[0:C, 0:1])
-
-    def li_scan(k):
-        scan(["nl%d" % k], "sl%d" % k, T["sl%d" % k][0:C, :], T["nl%d" % k][0:C, :], C)
-
-    def li_store(k):
-        act(["sl%d" % k], "li%d" % k, T["li%d" % k][0:C, 0:1], T["sl%d" % k][0:C, 127:128], F.Copy, scale=-1.0, bias=128.0)
-        dma("y", "dl%d" % k, ["li%d" % k], [], T.li[k:k + 1, 0:C], T["li%d" % k][0:C, 0:1])
-
-    ta = ("ta", ["ta"], 0)
-    scores("ur", *ta)
-    row(0, "p3", *ta)
-    compare("qh1")
-    quant("qv2", ["v1"], "qv", 256, T.vb[:, 1024:1536])
-    quant("qv3", ["v1"], "qv", 384, T.vb[:, 1536:2048])
-    old(0, "p4", *ta)
-    row(1, "p5", *ta)
-    pick_scales("up", ["ta", "rep0", "rep1"], *up)
-    relu(0, "p3", "ra")
-    relu(1, "p5", "ra")
-    ranks("qh1", "p1")
-    old(1, "p6", *ta)
-    row(2, "p7", *ta)
-    row(3, "p3", *ta)
-    old(2, "p0", *ta)
-    old(3, "p5", *ta)
-    relu(2, "p7", "ra")
-    relu(3, "p3", "ra")
-    add(0, "p4", "ra", "n1")
-    for k in range(2):
-        op("v", ["p1", "pa%d" % k], ["nb%d" % k], V.tensor_scalar, T.nb[:, 128 * k:128 * k + 128], T.p1[:, 0:128],
-           T["pa%d" % k][:, 0:1], 512.0, A.not_equal, A.mult)
-    add(1, "p6", "ra", "n1")
-    scan(["nb0"], "sc0", T.sc[:, 0:128], T.nb[:, 0:128])
-    add(2, "p0", "ra", "n1")
-    scan(["nb1"], "sc1", T.sc[:, 128:256], T.nb[:, 128:256])
-    add(3, "p5", "ra", "n1")
-    op("v", ["sc0", "sc1"], ["lst"], V.tensor_scalar, T.lst[:], T.sc[:, 127:256:128], -1.0, 128.0, A.mult, A.add)
-    quant("qn", ["n1%d" % i for i in range(4)], "qn", 0, T.n1[:])
-    pick("pk", ["qn", "lst"], "pk", 32, 0, "qn", 0, 128, T.lst[:, 0:2])
-    send(["pk"], nxt, code("tb", 0, C), code("pk", 0, 32), "arrn")
-    send(["pks"], nxt, T.tbs[:, 0:C], T.pks[:, 0:32], "arrn")
-
-    scores("up", "tb", ["tb"], C)
-    compare("qh2")
-    ranks("qh2", "p1")
-    ranks("qh2", "p2")
-    op("v", ["p1", "thr"], ["q1"], V.tensor_tensor, T.q1[:], T.p1[:, 0:128], T.thr[:], A.is_ge)
-    li_mark(0, "p2")
-    op("v", ["p1", "q1"], ["ml"], V.tensor_tensor, T.ml[:], T.p1[:, 0:128], T.q1[:], A.max)
-    op("v", ["cr", "ml"], ["r8"], V.tensor_tensor_scan, T.r8[:], T.cr[:], T.ml[:], 0.0, A.max, A.min)
-    op("v", ["r8"], ["off1"], V.tensor_scalar, T.off1[:], T.r8[:, 15:128:16], 256.0, None, A.mult)
-
-    pick("t1", ["tb", "tn", "off1"], "win", 128, 128, "tb", 0, 160, T.off1[:, 0:8])
-    t1 = ("win", ["t1", "t1s"], 128)
-    scores("ur", *t1)
-    row(0, "p3", *t1)
-    old(0, "p4", *t1)
-    row(1, "p5", *t1)
-    li_scan(0)
+    stop(1)
+    send(["t1"], code("win2", 128, 256), code("t1", 0, 128), "arr2", "all")
+    send(["t1s"], T.win2s[:, 128:256], T.t1s[:], "arr2", "all")
+    op("v", [], ["h2"], V.memset, T.h2[:], 0.0)
+    places(1)
+    send(["li1"], T.lr[:], T.li1[:], "arrl", "first")
     quant("qw", ["w"], "qw", 0, T.wb[:])
-    compare("qh3")
-    li_store(0)
-    relu(0, "p3", "rb")
-    relu(1, "p5", "rb")
-    ranks("qh3", "p1")
-    old(1, "p6", *t1)
-    row(2, "p7", *t1)
-    row(3, "p3", *t1)
-    old(2, "p0", *t1)
-    old(3, "p5", *t1)
-    ranks("qh3", "p2")
-    relu(2, "p7", "rb")
-    relu(3, "p3", "rb")
-    li_mark(1, "p2")
-    add(0, "p4", "rb", "n2")
-    op("v", ["p1", "thr"], ["fl"], V.tensor_tensor, T.fl[:], T.p1[:, 0:128], T.thr[:], A.is_lt)
-    add(1, "p6", "rb", "n2")
-    op("v", ["cb", "fl"], ["st"], V.tensor_tensor_scan, T.st[:], T.cb[:], T.fl[:], 0.0, A.max, A.subtract)
-    add(2, "p0", "rb", "n2")
-    add(3, "p5", "rb", "n2")
-    op("v", ["st"], ["off2"], V.tensor_scalar, T.off2[:], T.st[:, 15:128:16], 128.0, None, A.mult)
-    quant("n2q", ["n2%d" % i for i in range(4)], "win", 0, T.n2[:])
-    pick("t2", ["t1", "t1s", "n2q", "off2"], "t2", 128, 0, "win", 0, 256, T.off2[:, 0:8])
-    li_scan(1)
 
+    stop(2)
+
+    dma("y", "dl1", ["lr"], [], T.li[0:1, 0:C], T.lr[0:C, 0:1])
     mm(["qw", "t2", "t2s"], "p4", "qw", 0, "t2", 0)
     dma("y", "do", ["t2"], [], T.oc[:, 0:512], code("t2", 0, 128))
     op("v", ["p4"], ["ys"], V.tensor_copy, T.ys[:], T.p4[:, 0:128])
-    li_store(1)
     dma("s", "dy", ["ys"], [], T.y[:, 0:128], T.ys[:])
+    places(2)
     for k in range(4):
         dma("y", "ds%d" % k, ["t2s"], [], T.osc[4 * k:4 * k + 4, 0:128], T.t2s[32 * k:32 * k + 4, 0:128])
+    dma("y", "dl2", ["li2"], [], T.li[1:2, 0:C], T.li2[0:C, 0:1])
 
     for q in ("v", "s", "t", "g"):
         g.wait_ge(T.sem[counter[q]], count[q])

@@ -3,7 +3,7 @@ from concourse.mybir import dt, AluOpType, ActivationFunctionType
 N = 8
 C = 32
 FACTOR = 13421773 * 2.0 ** -28
-UNIT = 1.0 / 256
+FAR = 64.0
 TIE = 2.0 ** -100
 
 SCRATCH = {}
@@ -20,25 +20,28 @@ def _pair(width, *names):
         _declare("uint8", width, n + "s")
 
 
-_declare("bfloat16", 512, "xb", "ub", "wb", "wo", "h1", "h2", "n1", "n2")
+_declare("bfloat16", 512, "xb", "wb", "wo", "wp", "h1", "h2", "n1", "n2")
+_declare("bfloat16", 4, "ub")
+_declare("bfloat16", 1024, "uw")
 _declare("bfloat16", 2048, "vb")
 _declare("bfloat16", 520, "eb")
-_declare("bfloat16", 128, "ob", "zf", "idn", "tie", "dn", "jm", "far", "thr", "cb", "f1", "f2", "s1", "s2", "nl1", "nl2", "sl1", "sl2")
+_declare("bfloat16", 256, "ob")
+_declare("bfloat16", 128, "tie", "dn", "cb", "f1", "f2", "s1", "s2", "nl1", "nl2", "sl1", "sl2")
 _declare("float32", 128, "ys")
 _declare("float32", 512, "r1", "r2")
-_declare("float32", 1, "pif", "pm0", "pb", "pnp", "li1", "li2", "lr")
+_declare("float32", 1, "pm0", "pnp", "li1", "li2", "lr")
+_declare("float32", 4, "uf")
 _declare("float32", 8, "gs")
 _declare("int32", 1, "pii", "pmi")
-_declare("uint16", 16, "rep")
 _declare("uint16", 8, "off1", "off2")
 _pair(512, "qv", "qe")
 _pair(256, "win1", "win2")
 _pair(256, "ur")
-_pair(128, "qx", "qu", "qw", "qo", "qh1", "qh2", "t1", "t2")
+_pair(128, "qx", "qw", "qo", "qp", "qh1", "qh2", "t1", "t2")
 for _i in range(8):
     SCRATCH["p%d" % _i] = ("psum", [128, 512], "float32")
 
-LOADS = ["dx", "du", "dv0", "dv1", "dw"]
+LOADS = ["dx", "du", "dv", "dw"]
 STORES = ["do", "ds0", "ds1", "ds2", "ds3", "dy", "dl1", "dl2"]
 SEMAPHORES = ["cv", "cs", "ct", "cg", "sent", "arr1", "arr2", "arrl"] + LOADS + STORES
 
@@ -112,63 +115,64 @@ def rank_program(g, core, T, topo):
     def code(name, a, b):
         return T[name][:, a:b].bitcast(dt.uint8)
 
-    def quant(key, reads, name, a, in_):
-        op("v", reads, [key], V.quantize_mx, T[name][:, a:a + 128], T[name + "s"][:, a:a + 128], in_)
+    def quant(key, reads, name, a, in_, n=128):
+        op("v", reads, [key], V.quantize_mx, T[name][:, a:a + n], T[name + "s"][:, a:a + n], in_)
 
     def act(reads, key, out, in_, func, **kw):
         op("s", reads, [key], S.activation, out, in_, func, **kw)
 
-    def pick(key, reads, dst, n, src, a, b, off):
-        op("v", reads, [key], V.tensor_copy, T[dst][:, 0:n].bitcast(dt.uint32), T[src][:, a:b].bitcast(dt.uint32).indirect(off))
-        op("s", reads, [key + "s"], S.activation, T[dst + "s"][:, 0:n], T[src + "s"][:, a:b].indirect(off), F.Copy)
+    def pick(key, reads, dst, src, off):
+        op("v", reads, [key], V.tensor_copy, T[dst][:, 0:128].bitcast(dt.uint32), T[src][:, 0:256].bitcast(dt.uint32).indirect(off))
+        op("s", reads, [key + "s"], S.activation, T[dst + "s"][:, 0:128], T[src + "s"][:, 0:256].indirect(off), F.Copy)
 
     dma("y", "dx", [], ["x"], T.xb[:], T.x[:, 0:512])
-    dma("y", "du", [], ["u"], T.ub[:, 0:4], T.u[:, 0:4])
-    dma("y", "dv0", [], ["v0"], T.vb[:, 0:1024], T.v[:, 0:1024])
-    dma("y", "dv1", [], ["v1"], T.vb[:, 1024:2048], T.v[:, 1024:2048])
+    dma("y", "du", [], ["u"], T.ub[:], T.u[:, 0:4])
+    dma("y", "dv", [], ["v"], T.vb[:], T.v[:, 0:2048])
     dma("y", "dw", ["in1"], ["w"], T.wb[:], T.w[:, 0:512])
 
     small = dict(allow_small_or_imprecise_dtypes=True)
-    op("v", [], ["ob"], V.memset, T.ob[:], 1.0)
-    op("v", [], ["zf"], V.memset, T.zf[:], 0.0)
-    op("g", ["ob"], ["idn"], g.affine_select, T.idn[:], T.ob[:], [[-1, 128]], A.is_equal, 0.0, 0, 1)
-    op("g", [], ["pii"], g.iota, T.pii[:], [[0, 1]], 0, 1)
-    op("g", [], ["pif"], g.iota, T.pif[:], [[0, 1]], 0, 1, **small)
-    op("g", [], ["gs"], g.iota, T.gs[:], [[16, 8]], 128, 0, **small)
+    one = T.ob[:, 0:128]
+    wrap = [[0, 8], [-1, 16]]
+
+    def beside(k):
+        for t in (2, 3):
+            op("v", [], ["hz%d%d" % (k, t)], V.memset, T["h%d" % k][:, t:512:4], 0.0)
+
+    def agree(k):
+        op("g", ["ob"], ["hm%d" % k], g.affine_select, T["h%d" % k][:, 1:512:4], one, wrap, A.is_equal, 0.0, 0, 1)
+
+    op("v", [], ["ob"], V.memset, one, 1.0)
     op("v", [], ["eb"], V.memset, T.eb[:], 0.0)
-    op("v", [], ["h1"], V.memset, T.h1[:], 0.0)
-    op("v", [], ["rep0"], V.memset, T.rep[:, 0:8], 0)
-    op("v", [], ["rep1"], V.memset, T.rep[:, 8:16], 1)
-    op("v", ["idn"], ["eb"], V.tensor_copy, T.eb[:, 3:515:4], T.idn[:])
+    op("v", [], ["om"], V.memset, T.ob[:, 128:256], -1.0)
+    op("g", [], ["pii"], g.iota, T.pii[:], [[0, 1]], 0, 1)
+    op("g", [], ["gs"], g.iota, T.gs[:], [[1, 8]], 64, 0, **small)
+    op("g", ["ob", "eb"], ["e1"], g.affine_select, T.eb[:, 3:515:4], one, [[-1, 128]], A.is_equal, 0.0, 0, 1)
+    beside(1)
+    op("v", ["pii"], ["pmi"], V.tensor_scalar, T.pmi[:], T.pii[:], 15, None, A.bitwise_and)
+    op("v", ["pmi"], ["pm0"], V.tensor_copy, T.pm0[:], T.pmi[:])
+    for t in (0, 2, 3):
+        act(["ob"], "wo%d" % t, T.wo[:, t:512:4], one, F.Copy)
+    act(["ob"], "cb", T.cb[:], one, F.Copy, scale=0.0)
+    act(["gs"], "cb", T.cb[:, 0:128:16], T.gs[:], F.Copy, scale=0.25)
 
     quant("qx", ["x"], "qx", 0, T.xb[:])
-    send(["qx"], code("win1", 128, 256), code("qx", 0, 128), "arr1", "first")
-    send(["qx"], T.win1s[:, 128:256], T.qxs[:], "arr1", "last")
-    op("g", ["zf"], ["tie"], g.affine_select, T.tie[:], T.zf[:], [[-1, 128]], A.is_ge, TIE, 0, 1)
-    op("g", [], ["jm"], g.iota, T.jm[:], [[0, 8], [1, 16]], 0, 0, **small)
+    send(["qx"], code("win1", 0, 128), code("qx", 0, 128), "arr1", "first")
+    send(["qx"], T.win1s[:, 0:128], T.qxs[:], "arr1", "last")
+    op("g", ["ob"], ["wo1"], g.affine_select, T.wo[:, 1:512:4], one, wrap, A.is_equal, FAR, 0, 1)
+    op("g", ["hz12"], ["tie"], g.affine_select, T.tie[:], T.h1[:, 2:512:4], [[-1, 128]], A.is_ge, TIE, 0, 1)
+    agree(1)
+    op("g", [], ["pnp"], g.iota, T.pnp[:], [[0, 1]], -256, -256, **small)
     op("g", [], ["dn"], g.iota, T.dn[:], [[-1, 128]], 128, 0, **small)
 
-    for i in range(4):
-        a, b = max(8, 128 * i), 128 * i + 128
-        act(["ob"], "ub%d" % i, T.ub[:, a:b], T.ob[:, 0:b - a], F.Copy)
-    act(["u"], "nu", T.ub[:, 4:8], T.ub[:, 0:4], F.Copy, scale=-1.0)
-    for i in range(4):
-        act(["ob"], "wo%d" % i, T.wo[:, 128 * i:128 * i + 128], T.ob[:], F.Copy, scale=UNIT)
-    quant("qu", ["u", "nu"] + ["ub%d" % i for i in range(4)], "qu", 0, T.ub[:])
-    pick("ur", ["qu", "rep0", "rep1"], "ur", 256, "qu", 0, 2, T.rep[:, 0:16])
-    op("v", ["pii"], ["pmi"], V.tensor_scalar, T.pmi[:], T.pii[:], 15, None, A.bitwise_and)
+    act(["u"], "uf", T.uf[:], T.ub[:], F.Copy)
+    for t in range(4):
+        act(["ob", "om", "uf"], "uw%d" % t, T.uw[:, t:1024:4], T.ob[:], F.Identity, scale=T.uf[:, t:t + 1])
     for b in range(4):
-        quant("qe%d" % b, ["eb"], "qe", 128 * b, T.eb[:, 3 - b:515 - b])
-    op("v", ["pmi"], ["pm0"], V.tensor_copy, T.pm0[:], T.pmi[:])
-    quant("qo", ["wo%d" % i for i in range(4)], "qo", 0, T.wo[:])
-    for i in range(4):
-        quant("qv%d" % i, ["v%d" % (i // 2)], "qv", 128 * i, T.vb[:, 512 * i:512 * i + 512])
-    act(["pif"], "pnp", T.pnp[:], T.pif[:], F.Copy, scale=-256.0)
-    act(["pm0"], "pb", T.pb[:], T.pm0[:], F.Copy, scale=1.0 / 128)
-    act(["jm", "pm0"], "far", T.far[:], T.jm[:], F.Abs, scale=-1.0, bias=T.pm0[:, 0:1])
-    act(["far"], "thr", T.thr[:], T.far[:], F.Relu, scale=-C * UNIT, bias=C * UNIT)
-    act(["zf"], "cb", T.cb[:], T.zf[:], F.Copy, bias=-1.0)
-    act(["gs", "pb"], "cb", T.cb[:, 0:128:16], T.gs[:], F.Identity, scale=1.0 / 128, bias=T.pb[:, 0:1])
+        quant("qe%d" % b, ["eb", "e1"], "qe", 128 * b, T.eb[:, 3 - b:515 - b])
+    quant("qo", ["wo%d" % t for t in range(4)], "qo", 0, T.wo[:])
+    quant("ur", ["uw%d" % t for t in range(4)], "ur", 0, T.uw[:], 256)
+    for i in range(2):
+        quant("qv%d" % i, ["v"], "qv", 256 * i, T.vb[:, 1024 * i:1024 * i + 1024], 256)
 
     def mm(reads, bank, w, a, x, b):
         op("t", reads, [bank], E.matmul_mx, T[bank][:, 0:128], T[w][:, a:a + 128], T[w + "s"][:, a:a + 128],
@@ -176,47 +180,51 @@ def rank_program(g, core, T, topo):
 
     def stop(k):
         win, key, n, r, qh, h = "win%d" % k, "in%d" % k, "n%d" % k, "r%d" % k, "qh%d" % k, "h%d" % k
-        flag, state, off, nl = "f%d" % k, "s%d" % k, "off%d" % k, "nl%d" % k
+        flag, state, off = "f%d" % k, "s%d" % k, "off%d" % k
 
         def row(i, bank):
-            mm(["qv%d" % i, key], bank, "qv", 128 * i, win, 128)
+            mm(["qv%d" % (i // 2), key], bank, "qv", 128 * i, win, 0)
             act([bank], r + str(i), T[r][:, 128 * i:128 * i + 128], T[bank][:, 0:128], F.Relu, scale=FACTOR)
 
         def old(i, bank):
-            mm(["qe%d" % i, key], bank, "qe", 128 * i, win, 128)
+            mm(["qe%d" % i, key], bank, "qe", 128 * i, win, 0)
 
         def add(i, bank):
             op("v", [bank, r + str(i)], [n + str(i)], V.tensor_tensor, T[n][:, i:512:4], T[bank][:, 0:128],
                T[r][:, 128 * i:128 * i + 128], A.add)
 
-        reads = ["ur", "urs", key]
+        reads = ["ur", key]
         ready("t", reads, ["p0"])
-        issue("t", reads, ["p0"], E.matmul_mx, T.p0[:, 0:128], T[win][:, 128:256], T[win + "s"][:, 128:256],
+        issue("t", reads, ["p0"], E.matmul_mx, T.p0[:, 0:128], T[win][:, 0:128], T[win + "s"][:, 0:128],
               T.ur[:, 128:256], T.urs[:, 128:256], True, False)
         issue("t", reads, ["p0"], E.matmul_mx, T.p0[:, 0:128], T.ur[:, 0:128], T.urs[:, 0:128],
-              T[win][:, 128:256], T[win + "s"][:, 128:256], False, True)
+              T[win][:, 0:128], T[win + "s"][:, 0:128], False, True)
+        op("v", ["tie", "p0"], [h], V.tensor_tensor, T[h][:, 0:512:4], T.p0[:, 0:128], T.tie[:], A.is_lt)
+        quant(qh, [h, "hm%d" % k, "hz%d2" % k, "hz%d3" % k], qh, 0, T[h][:])
         row(0, "p3")
         old(0, "p4")
         row(1, "p5")
-        op("v", ["tie", "p0"], [h], V.tensor_tensor, T[h][:, 0:512:4], T.p0[:, 0:128], T.tie[:], A.is_lt)
-        quant(qh, [h], qh, 0, T[h][:])
-        mm(["qo", qh], "p1", "qo", 0, qh, 0)
-        old(1, "p6")
         row(2, "p7")
-        row(3, "p3")
-        old(2, "p0")
-        old(3, "p5")
-        mm(["qo", qh], "p2", "qo", 0, qh, 0)
+        old(1, "p6")
+        row(3, "p2")
+        old(2, "p3")
+        mm(["qo", qh], "p1", "qo", 0, qh, 0)
+        act(["p1"], flag, T[flag][:], T.p1[:, 0:128], F.Sign, bias=-0.5 - C)
+        old(3, "p0")
         add(0, "p4")
-        op("v", ["p1", "thr"], [flag], V.tensor_tensor, T[flag][:], T.p1[:, 0:128], T.thr[:], A.is_lt)
         add(1, "p6")
+        add(2, "p3")
+        add(3, "p0")
         op("v", ["cb", flag], [state], V.tensor_tensor_scan, T[state][:], T.cb[:], T[flag][:], 0.0, A.max, A.subtract)
-        add(2, "p0")
-        add(3, "p5")
-        op("v", [state], [off], V.tensor_scalar, T[off][:], T[state][:, 15:128:16], 128.0, None, A.mult)
-        quant("q" + n, [n + str(i) for i in range(4)], win, 0, T[n][:])
-        pick("t%d" % k, [key, "q" + n, off], "t%d" % k, 128, win, 0, 256, T[off][:])
-        act(["p2", "pnp"], nl, T[nl][:], T.p2[:, 0:128], F.Abs, scale=65536.0, bias=T.pnp[:, 0:1])
+        quant("q" + n, [n + str(i) for i in range(4)], win, 128, T[n][:])
+        op("v", [state, "pm0"], [off], V.tensor_scalar, T[off][:], T[state][:, 15:128:16], 64.0, T.pm0[:, 0:1], A.mult, A.add)
+        if k == 2:
+            ranks(k)
+        pick("t%d" % k, [key, "q" + n, off], "t%d" % k, win, T[off][:])
+
+    def ranks(k):
+        mm(["qp", "qh%d" % k], "p5", "qp", 0, "qh%d" % k, 0)
+        act(["p5", "pnp"], "nl%d" % k, T["nl%d" % k][:], T.p5[:, 0:128], F.Abs, scale=256.0, bias=T.pnp[:, 0:1])
 
     def places(k):
         nl, sl, li = "nl%d" % k, "sl%d" % k, "li%d" % k
@@ -224,9 +232,13 @@ def rank_program(g, core, T, topo):
         act([sl], li, T[li][:], T[sl][:, 127:128], F.Copy, scale=-1.0, bias=128.0)
 
     stop(1)
-    send(["t1"], code("win2", 128, 256), code("t1", 0, 128), "arr2", "all")
-    send(["t1s"], T.win2s[:, 128:256], T.t1s[:], "arr2", "all")
-    op("v", [], ["h2"], V.memset, T.h2[:], 0.0)
+    send(["t1"], code("win2", 0, 128), code("t1", 0, 128), "arr2", "all")
+    send(["t1s"], T.win2s[:, 0:128], T.t1s[:], "arr2", "all")
+    agree(2)
+    op("v", [], ["wp"], V.memset, T.wp[:], 1.0)
+    quant("qp", ["wp"], "qp", 0, T.wp[:])
+    beside(2)
+    ranks(1)
     places(1)
     send(["li1"], T.lr[:], T.li1[:], "arrl", "first")
     quant("qw", ["w"], "qw", 0, T.wb[:])
@@ -234,13 +246,13 @@ def rank_program(g, core, T, topo):
     stop(2)
 
     dma("y", "dl1", ["lr"], [], T.li[0:1, 0:C], T.lr[0:C, 0:1])
-    mm(["qw", "t2", "t2s"], "p4", "qw", 0, "t2", 0)
     dma("y", "do", ["t2"], [], T.oc[:, 0:512], code("t2", 0, 128))
+    mm(["qw", "t2", "t2s"], "p4", "qw", 0, "t2", 0)
+    for k in range(4):
+        dma("yyss"[k], "ds%d" % k, ["t2s"], [], T.osc[4 * k:4 * k + 4, 0:128], T.t2s[32 * k:32 * k + 4, 0:128])
+    places(2)
     op("v", ["p4"], ["ys"], V.tensor_copy, T.ys[:], T.p4[:, 0:128])
     dma("s", "dy", ["ys"], [], T.y[:, 0:128], T.ys[:])
-    places(2)
-    for k in range(4):
-        dma("y", "ds%d" % k, ["t2s"], [], T.osc[4 * k:4 * k + 4, 0:128], T.t2s[32 * k:32 * k + 4, 0:128])
     dma("y", "dl2", ["li2"], [], T.li[1:2, 0:C], T.li2[0:C, 0:1])
 
     for q in ("v", "s", "t", "g"):

from concourse.mybir import dt, AluOpType, ActivationFunctionType

N = 8
C = 32
FACTOR = 13421773 * 2.0 ** -28
FAR = 64.0
TIE = 2.0 ** -100

SCRATCH = {}


def _declare(kind, width, *names):
    for n in names:
        SCRATCH[n] = ("sbuf", [128, width], kind)


def _pair(width, *names):
    for n in names:
        _declare("float8_e4m3fn_x4", width, n)
        _declare("uint8", width, n + "s")


_declare("bfloat16", 512, "xb", "wb", "wo", "wp", "h1", "h2", "n1", "n2")
_declare("bfloat16", 4, "ub")
_declare("bfloat16", 1024, "uw")
_declare("bfloat16", 2048, "vb")
_declare("bfloat16", 520, "eb")
_declare("bfloat16", 256, "ob")
_declare("bfloat16", 128, "tie", "dn", "cb", "f1", "f2", "s1", "s2", "nl1", "nl2", "sl1", "sl2")
_declare("float32", 128, "ys")
_declare("float32", 512, "r1", "r2")
_declare("float32", 1, "pm0", "pnp", "li1", "li2", "lr")
_declare("float32", 4, "uf")
_declare("float32", 8, "gs")
_declare("int32", 1, "pii", "pmi")
_declare("uint16", 8, "off1", "off2")
_pair(512, "qv", "qe")
_pair(256, "win1", "win2")
_pair(256, "ur")
_pair(128, "qx", "qw", "qo", "qp", "qh1", "qh2", "t1", "t2")
for _i in range(8):
    SCRATCH["p%d" % _i] = ("psum", [128, 512], "float32")

LOADS = ["dx", "du", "dv", "dw"]
STORES = ["do", "ds0", "ds1", "ds2", "ds3", "dy", "dl1", "dl2"]
SEMAPHORES = ["cv", "cs", "ct", "cg", "sent", "arr1", "arr2", "arrl"] + LOADS + STORES


def rank_program(g, core, T, topo):
    rank = T.rank_of(core)
    if rank is None:
        return
    A, F = AluOpType, ActivationFunctionType
    queue = {"v": g.vector, "s": g.scalar, "t": g.tensor, "g": g, "y": g.sync}
    counter = {"v": "cv", "s": "cs", "t": "ct", "g": "cg"}
    count = {"v": 0, "s": 0, "t": 0, "g": 0}
    known = {q: {} for q in queue}
    wrote, read = {}, {}
    order = [0]

    def ready(q, reads, writes):
        need = [wrote[k] for k in list(reads) + list(writes) if k in wrote]
        for k in writes:
            need += read.get(k, [])
        for _, name, val, kn in sorted(need, key=lambda e: -e[0]):
            if known[q].get(name, 0) < val:
                queue[q].wait_ge(T.sem[name], val)
                known[q][name] = val
            for n2, v2 in kn.items():
                known[q][n2] = max(known[q].get(n2, 0), v2)

    def done(q, ev, reads, writes):
        for k in reads:
            read.setdefault(k, []).append(ev)
        for k in writes:
            wrote[k] = ev
            read[k] = []

    def issue(q, reads, writes, call, *args, **kw):
        count[q] += 1
        order[0] += 1
        call(*args, **kw).then_inc(T.sem[counter[q]], 1)
        done(q, (order[0], counter[q], count[q], dict(known[q])), reads, writes)

    def op(q, reads, writes, call, *args, **kw):
        ready(q, reads, writes)
        issue(q, reads, writes, call, *args, **kw)

    def dma(q, sem, reads, writes, out, in_):
        ready(q, reads, writes)
        order[0] += 1
        queue[q].dma_start(out, in_).then_inc(T.sem[sem], 16)
        done(q, (order[0], sem, 16, dict(known[q])), reads, writes)

    V, S, E = g.vector, g.scalar, g.tensor
    nxt, prv = T.cores[(rank + 1) % N], T.cores[(rank - 1) % N]

    def lanes(src, dst, part):
        es = topo.engines(src, dst)
        return {"first": es[:8], "last": es[-8:], "all": es}[part]

    sent = [0]

    def send(reads, out, in_, sem, part):
        ready("g", reads, [])
        rid, pid = topo.addr(nxt, core)
        es = lanes(core, nxt, part)
        sent[0] += len(es)
        g.remote_dma(out_ap=out, in_ap=in_, remote_sem=T.sem[sem], local_sem=T.sem.sent, pid=pid, routing_id=rid,
                     dma_engine_mask=sum(1 << e for e in es))

    for key, sem, parts in (("in1", "arr1", ("first", "last")), ("in2", "arr2", ("all", "all")), ("lr", "arrl", ("first",))):
        wrote[key] = (0, sem, sum(len(lanes(prv, core, p)) for p in parts), {})

    def code(name, a, b):
        return T[name][:, a:b].bitcast(dt.uint8)

    def quant(key, reads, name, a, in_, n=128):
        op("v", reads, [key], V.quantize_mx, T[name][:, a:a + n], T[name + "s"][:, a:a + n], in_)

    def act(reads, key, out, in_, func, **kw):
        op("s", reads, [key], S.activation, out, in_, func, **kw)

    def pick(key, reads, dst, src, off):
        op("v", reads, [key], V.tensor_copy, T[dst][:, 0:128].bitcast(dt.uint32), T[src][:, 0:256].bitcast(dt.uint32).indirect(off))
        op("s", reads, [key + "s"], S.activation, T[dst + "s"][:, 0:128], T[src + "s"][:, 0:256].indirect(off), F.Copy)

    dma("y", "dx", [], ["x"], T.xb[:], T.x[:, 0:512])
    dma("y", "du", [], ["u"], T.ub[:], T.u[:, 0:4])
    dma("y", "dv", [], ["v"], T.vb[:], T.v[:, 0:2048])
    dma("y", "dw", ["in1"], ["w"], T.wb[:], T.w[:, 0:512])

    small = dict(allow_small_or_imprecise_dtypes=True)
    one = T.ob[:, 0:128]
    wrap = [[0, 8], [-1, 16]]

    def beside(k):
        for t in (2, 3):
            op("v", [], ["hz%d%d" % (k, t)], V.memset, T["h%d" % k][:, t:512:4], 0.0)

    def agree(k):
        op("g", ["ob"], ["hm%d" % k], g.affine_select, T["h%d" % k][:, 1:512:4], one, wrap, A.is_equal, 0.0, 0, 1)

    op("v", [], ["ob"], V.memset, one, 1.0)
    op("v", [], ["eb"], V.memset, T.eb[:], 0.0)
    op("v", [], ["om"], V.memset, T.ob[:, 128:256], -1.0)
    op("g", [], ["pii"], g.iota, T.pii[:], [[0, 1]], 0, 1)
    op("g", [], ["gs"], g.iota, T.gs[:], [[1, 8]], 64, 0, **small)
    op("g", ["ob", "eb"], ["e1"], g.affine_select, T.eb[:, 3:515:4], one, [[-1, 128]], A.is_equal, 0.0, 0, 1)
    beside(1)
    op("v", ["pii"], ["pmi"], V.tensor_scalar, T.pmi[:], T.pii[:], 15, None, A.bitwise_and)
    op("v", ["pmi"], ["pm0"], V.tensor_copy, T.pm0[:], T.pmi[:])
    for t in (0, 2, 3):
        act(["ob"], "wo%d" % t, T.wo[:, t:512:4], one, F.Copy)
    act(["ob"], "cb", T.cb[:], one, F.Copy, scale=0.0)
    act(["gs"], "cb", T.cb[:, 0:128:16], T.gs[:], F.Copy, scale=0.25)

    quant("qx", ["x"], "qx", 0, T.xb[:])
    send(["qx"], code("win1", 0, 128), code("qx", 0, 128), "arr1", "first")
    send(["qx"], T.win1s[:, 0:128], T.qxs[:], "arr1", "last")
    op("g", ["ob"], ["wo1"], g.affine_select, T.wo[:, 1:512:4], one, wrap, A.is_equal, FAR, 0, 1)
    op("g", ["hz12"], ["tie"], g.affine_select, T.tie[:], T.h1[:, 2:512:4], [[-1, 128]], A.is_ge, TIE, 0, 1)
    agree(1)
    op("g", [], ["pnp"], g.iota, T.pnp[:], [[0, 1]], -256, -256, **small)
    op("g", [], ["dn"], g.iota, T.dn[:], [[-1, 128]], 128, 0, **small)

    act(["u"], "uf", T.uf[:], T.ub[:], F.Copy)
    for t in range(4):
        act(["ob", "om", "uf"], "uw%d" % t, T.uw[:, t:1024:4], T.ob[:], F.Identity, scale=T.uf[:, t:t + 1])
    for b in range(4):
        quant("qe%d" % b, ["eb", "e1"], "qe", 128 * b, T.eb[:, 3 - b:515 - b])
    quant("qo", ["wo%d" % t for t in range(4)], "qo", 0, T.wo[:])
    quant("ur", ["uw%d" % t for t in range(4)], "ur", 0, T.uw[:], 256)
    for i in range(2):
        quant("qv%d" % i, ["v"], "qv", 256 * i, T.vb[:, 1024 * i:1024 * i + 1024], 256)

    def mm(reads, bank, w, a, x, b):
        op("t", reads, [bank], E.matmul_mx, T[bank][:, 0:128], T[w][:, a:a + 128], T[w + "s"][:, a:a + 128],
           T[x][:, b:b + 128], T[x + "s"][:, b:b + 128], True, True)

    def stop(k):
        win, key, n, r, qh, h = "win%d" % k, "in%d" % k, "n%d" % k, "r%d" % k, "qh%d" % k, "h%d" % k
        flag, state, off = "f%d" % k, "s%d" % k, "off%d" % k

        def row(i, bank):
            mm(["qv%d" % (i // 2), key], bank, "qv", 128 * i, win, 0)
            act([bank], r + str(i), T[r][:, 128 * i:128 * i + 128], T[bank][:, 0:128], F.Relu, scale=FACTOR)

        def old(i, bank):
            mm(["qe%d" % i, key], bank, "qe", 128 * i, win, 0)

        def add(i, bank):
            op("v", [bank, r + str(i)], [n + str(i)], V.tensor_tensor, T[n][:, i:512:4], T[bank][:, 0:128],
               T[r][:, 128 * i:128 * i + 128], A.add)

        reads = ["ur", key]
        ready("t", reads, ["p0"])
        issue("t", reads, ["p0"], E.matmul_mx, T.p0[:, 0:128], T[win][:, 0:128], T[win + "s"][:, 0:128],
              T.ur[:, 128:256], T.urs[:, 128:256], True, False)
        issue("t", reads, ["p0"], E.matmul_mx, T.p0[:, 0:128], T.ur[:, 0:128], T.urs[:, 0:128],
              T[win][:, 0:128], T[win + "s"][:, 0:128], False, True)
        op("v", ["tie", "p0"], [h], V.tensor_tensor, T[h][:, 0:512:4], T.p0[:, 0:128], T.tie[:], A.is_lt)
        quant(qh, [h, "hm%d" % k, "hz%d2" % k, "hz%d3" % k], qh, 0, T[h][:])
        row(0, "p3")
        old(0, "p4")
        row(1, "p5")
        row(2, "p7")
        old(1, "p6")
        row(3, "p2")
        old(2, "p3")
        mm(["qo", qh], "p1", "qo", 0, qh, 0)
        act(["p1"], flag, T[flag][:], T.p1[:, 0:128], F.Sign, bias=-0.5 - C)
        old(3, "p0")
        add(0, "p4")
        add(1, "p6")
        add(2, "p3")
        add(3, "p0")
        op("v", ["cb", flag], [state], V.tensor_tensor_scan, T[state][:], T.cb[:], T[flag][:], 0.0, A.max, A.subtract)
        quant("q" + n, [n + str(i) for i in range(4)], win, 128, T[n][:])
        op("v", [state, "pm0"], [off], V.tensor_scalar, T[off][:], T[state][:, 15:128:16], 64.0, T.pm0[:, 0:1], A.mult, A.add)
        if k == 2:
            ranks(k)
        pick("t%d" % k, [key, "q" + n, off], "t%d" % k, win, T[off][:])

    def ranks(k):
        mm(["qp", "qh%d" % k], "p5", "qp", 0, "qh%d" % k, 0)
        act(["p5", "pnp"], "nl%d" % k, T["nl%d" % k][:], T.p5[:, 0:128], F.Abs, scale=256.0, bias=T.pnp[:, 0:1])

    def places(k):
        nl, sl, li = "nl%d" % k, "sl%d" % k, "li%d" % k
        op("v", [nl, "dn"], [sl], V.tensor_tensor_scan, T[sl][:], T[nl][:], T.dn[:], 200.0, A.min, A.max)
        act([sl], li, T[li][:], T[sl][:, 127:128], F.Copy, scale=-1.0, bias=128.0)

    stop(1)
    send(["t1"], code("win2", 0, 128), code("t1", 0, 128), "arr2", "all")
    send(["t1s"], T.win2s[:, 0:128], T.t1s[:], "arr2", "all")
    agree(2)
    op("v", [], ["wp"], V.memset, T.wp[:], 1.0)
    quant("qp", ["wp"], "qp", 0, T.wp[:])
    beside(2)
    ranks(1)
    places(1)
    send(["li1"], T.lr[:], T.li1[:], "arrl", "first")
    quant("qw", ["w"], "qw", 0, T.wb[:])

    stop(2)

    dma("y", "dl1", ["lr"], [], T.li[0:1, 0:C], T.lr[0:C, 0:1])
    dma("y", "do", ["t2"], [], T.oc[:, 0:512], code("t2", 0, 128))
    mm(["qw", "t2", "t2s"], "p4", "qw", 0, "t2", 0)
    for k in range(4):
        dma("yyss"[k], "ds%d" % k, ["t2s"], [], T.osc[4 * k:4 * k + 4, 0:128], T.t2s[32 * k:32 * k + 4, 0:128])
    places(2)
    op("v", ["p4"], ["ys"], V.tensor_copy, T.ys[:], T.p4[:, 0:128])
    dma("s", "dy", ["ys"], [], T.y[:, 0:128], T.ys[:])
    dma("y", "dl2", ["li2"], [], T.li[1:2, 0:C], T.li2[0:C, 0:1])

    for q in ("v", "s", "t", "g"):
        g.wait_ge(T.sem[counter[q]], count[q])
    for s in LOADS + STORES:
        g.wait_ge(T.sem[s], 16)
    g.wait_ge(T.sem.sent, sent[0])
